import numpy as np, ml_dtypes
CORES = [16,17,18,19,32,33,34,35]
N = 8
BF = ml_dtypes.bfloat16
def gentries(a):
    return np.ascontiguousarray(a.reshape(8, 16, -1).transpose(0, 2, 1)).reshape(8, -1)
def gtable(e):
    e = np.asarray(e); return np.ascontiguousarray(e.reshape(8, -1, 16).transpose(0, 2, 1)).reshape(128, -1).astype(np.int32)
W, MA, J, P, T = 4096, 128, 768, 3, 3
def lanes(rng, big=False):
    jm = np.zeros((N, 8, MA), np.int64); lab = np.zeros((N, 8, J), np.int64); nx = np.zeros((N, 8, 16, J), np.int64)
    for q in range(N):
        for g in range(8):
            o = rng.permutation(J); p = rng.permutation(MA)
            tail = p[(MA * rng.random(J - MA) ** 2).astype(np.int64)]
            if big: tail[:] = p[0]
            lb = np.concatenate([np.arange(MA), tail]); s = np.argsort(lb, kind="stable"); cnt = np.bincount(lb, minlength=MA); st = np.add.accumulate(cnt) - cnt
            jm[q, g] = o[:MA]; lab[q, g, o] = lb
            nx[q, g][:, o] = o[s[st[lb] + (cnt[lb] * rng.random((16, J))).astype(np.int64)]]
            if big:
                pos = np.zeros(J, np.int64); pos[s] = np.arange(J) - st[lb[s]]
                nx[q, g][:8, o] = o[s[st[lb] + (pos + 1) % cnt[lb]]]
    return jm, lab, nx
def parts(rng, big=False):
    jm, lab, nx = lanes(rng, big); pal = rng.integers(0, W, (8, 16, MA, 6))
    ga = np.arange(8)[None, :, None, None]; ka = np.arange(16)[None, None, :, None]
    tool = np.where(rng.random((N, 8, 16, J)) < 0.75, pal[ga, ka, lab[:, :, None, :], rng.integers(0, 6, (N, 8, 16, J))], rng.integers(0, W, (N, 8, 16, J)))
    sh = (N, 8, 16, P, MA)
    name = np.where(rng.random(sh) < 0.8, pal[ga[..., None], ka[..., None], np.arange(MA), rng.integers(0, 6, sh)], rng.integers(0, W, sh))
    x = np.clip(rng.integers(0, 256, (N, 8, 1, W)) + rng.integers(-64, 65, (N, 8, 16, W)), 0, 255)
    lm = np.clip(rng.integers(64, 257, (N, 8, 1, J)) + rng.integers(-48, 49, (N, 8, 16, J)), 0, 255)
    return {"jm": jm, "nx": nx, "tool": tool, "name": name, "f": rng.integers(0, J, sh), "x": x, "lm": lm, "sd": rng.integers(0, 256, (N, 8, 16, W)), "rt": rng.integers(0, 65, (N, 8, 16, T))}
def full(a):
    return np.ascontiguousarray(a.reshape(N, 128, -1))
def pack(v):
    b = {k: full(v[k]).astype(np.float32).astype(BF) for k in ("x", "sd", "lm", "rt")}
    return {"xw": b["x"], "sd": b["sd"], "jt": full(4096 * v["nx"] + v["tool"]).astype(np.int32), "lm": b["lm"], "rt": b["rt"],
            "pk": full(4096 * v["f"] + v["name"]).astype(np.int32), "jm": np.stack([gtable(a) for a in v["jm"]])}
def setup_inputs(rng):
    return pack(parts(rng))
def setup_inputs_ties(rng):
    v = parts(rng)
    n = rng.choice(np.array([0, 7, 8, 9, 10, 16]), (N, 8, 1, W)); r = np.argsort(rng.random((N, 8, 16, W)), axis=2)
    v["x"] = 100 + (r < n).astype(np.int64); v["lm"] = np.full((N, 8, 16, J), 100); v["rt"] = rng.integers(0, 3, (N, 8, 16, T))
    v["f"] = rng.choice(np.array([0, J // 2, J - 1]), (N, 8, 16, P, MA))
    v["name"][:, :, :, 1] = np.where(rng.random((N, 8, 16, MA)) < 0.5, v["name"][:, :, :, 0], v["name"][:, :, :, 1])
    return pack(v)
def setup_inputs_crowd(rng):
    v = parts(rng); few = rng.integers(0, W, (8, 24)); ga = np.arange(8)[None, :, None, None]; m = np.arange(MA)
    v["tool"] = few[ga, rng.integers(0, 24, (N, 8, 16, J))]; v["name"] = few[ga[..., None], rng.integers(0, 24, (N, 8, 16, P, MA))]
    v["x"] = rng.choice(np.array([0, 3, 7, 8, 9, 128, 250, 254, 255]), (N, 8, 16, W)); v["rt"] = rng.choice(np.array([0, 1, 5, 64]), (N, 8, 16, T))
    other = np.setdiff1d(np.arange(W), few)
    for q in range(N):
        o = rng.permutation(8)
        g = o[0]; c, d = rng.permutation(other)[:2]
        v["lm"][q, g] = 255; v["tool"][q, g] = d; v["name"][q, g] = c; v["f"][q, g][:, 0] = J - 1; v["x"][q, g][:, c] = rng.integers(32, 256, 16)
        for g, w in ((o[1], 0), (o[2], 255)):
            c, d, e = rng.permutation(other)[:3]; m0 = int(rng.integers(1, 9))
            nm = np.where(m < m0, e, c); goes = (m == m0) == (w == 0)
            v["lm"][q, g] = 255; v["x"][q, g] = w; v["name"][q, g][0] = nm
            v["tool"][q, g][0, v["jm"][q, g]] = np.where(goes, nm, d)
            v["rt"][q, g] = rng.integers(17, 65, (16, T)) if w == 0 else rng.integers(0, 3, (16, T))
        g = o[3]; a = rng.permutation(W)[:17]; k0 = rng.integers(1, 8, MA)
        v["x"][q, g][:, a[0]] = rng.integers(0, 150, 16)
        v["x"][q, g][:, a[1:]] = rng.permuted(np.tile(rng.integers(150, 256, (16, 1)), (1, 16)), axis=0)
        v["tool"][q, g][:, v["jm"][q, g]] = np.where(np.arange(16)[:, None] < k0[None, :], a[0], a[1:][:, None])
    return pack(v)
def setup_inputs_ends(rng):
    v = parts(rng, True); e = np.array([0, 1, W - 2, W - 1])
    v["tool"] = np.where(rng.random((N, 8, 16, J)) < 0.5, rng.choice(e, (N, 8, 16, J)), v["tool"])
    v["name"] = np.where(rng.random((N, 8, 16, P, MA)) < 0.5, rng.choice(e, (N, 8, 16, P, MA)), v["name"])
    v["sd"] = np.where(rng.random((N, 8, 16, W)) < 0.5, rng.choice(np.array([0, 1, 255]), (N, 8, 16, W)), v["sd"])
    v["f"] = np.where(rng.random((N, 8, 16, P, MA)) < 0.5, rng.choice(np.array([0, J - 1]), (N, 8, 16, P, MA)), v["f"])
    return pack(v)
def setup_inputs_calm(rng):
    v = parts(rng); q = rng.permutation(N)
    v["lm"][q[0]] = 255; a = np.take_along_axis(v["tool"][q[0]], v["jm"][q[0]][:, None, :], 2)
    np.put_along_axis(v["name"][q[0]], rng.integers(0, P, (8, 16, 1, MA)), a[:, :, None, :], 2)
    v["lm"][q[1]] = 0; v["x"][q[1]] = np.maximum(v["x"][q[1]], 1)
    v["tool"][q[2]] = 2 * (v["tool"][q[2]] // 2); v["sd"][q[2]] = 2 * (v["sd"][q[2]] // 2); v["name"][q[2]] = 2 * (v["name"][q[2]] // 2) + 1
    return pack(v)
def setup_inputs_spread(rng):
    v = parts(rng)
    v["x"] = np.minimum((np.exp2(8 * rng.random((N, 8, 1, W))) * rng.random((N, 8, 16, W))).astype(np.int64), 255)
    v["lm"] = np.minimum((np.exp2(8 * rng.random((N, 8, 1, J))) * rng.random((N, 8, 16, J))).astype(np.int64), 255)
    v["rt"] = np.minimum(np.exp2(6 * rng.random((N, 8, 16, T))).astype(np.int64), 64)
    v["sd"] = np.minimum(np.exp2(8 * rng.random((N, 8, 16, W))).astype(np.int64), 255)
    v["tool"] = np.where(rng.random((N, 8, 16, J)) < 0.5, np.minimum((W * rng.random((N, 8, 16, J)) ** 3).astype(np.int64), W - 1), v["tool"])
    v["f"] = np.minimum((J * rng.random((N, 8, 16, P, MA)) ** 3).astype(np.int64), J - 1)
    return pack(v)
def check_inputs(d):
    bad = []
    for k, hi in (("xw", 255), ("sd", 255), ("lm", 255), ("rt", 64)):
        v = np.asarray(d[k]).astype(np.float64)
        if not np.all((v >= 0) & (v <= hi) & (v == np.floor(v))): bad.append("range of " + k)
    for k in ("jt", "pk"):
        v = np.asarray(d[k]).astype(np.int64)
        if np.min(v) < 0 or np.max(v) > 4096 * J - 1 or np.max(v & 4095) > W - 1: bad.append("range of " + k)
    if np.min(d["jm"]) < 0 or np.max(d["jm"]) > J - 1: bad.append("range of jm")
    if bad: return bad
    ok = True; nx = np.asarray(d["jt"]).astype(np.int64).reshape(N, 8, 16, J) >> 12
    for q in range(N):
        starts = gentries(np.asarray(d["jm"][q])).astype(np.int64)
        for g in range(8):
            fr = starts[g]; lab = np.full(J, -1)
            if len(np.unique(fr)) < MA: ok = False; continue
            lab[fr] = np.arange(MA)
            while len(fr):
                tg = nx[q, g][:, fr].reshape(-1); lb = np.tile(lab[fr], 16); new = lab[tg] < 0
                lab[tg[new]] = lb[new]
                if np.any(lab[tg] != lb): ok = False; break
                fr = np.unique(tg[new])
    if not ok: bad.append("lanes: a job can be reached from the starting jobs of two machines")
    return bad
def reference(xw, sd, jt, lm, rt, pk, jm):
    x = xw.astype(np.int64).reshape(N, 8, 16, W); s = sd.astype(np.int64).reshape(N, 8, 16, W); lim = lm.astype(np.int64).reshape(N, 8, 16, J); wr = rt.astype(np.int64).reshape(N, 8, 16, T)
    tab = jt.astype(np.int64).reshape(N, 8, 16, J); p = pk.astype(np.int64).reshape(N, 8, 16, P, MA)
    j = np.stack([gentries(a) for a in jm]).astype(np.int64)
    qa = np.arange(N)[:, None, None]; ga = np.arange(8)[None, :, None]
    for t in range(T):
        jj = np.ascontiguousarray(np.broadcast_to(j[:, :, None, :], (N, 8, 16, MA)))
        rec = np.take_along_axis(tab, jj, 3); a = rec & 4095; n = rec >> 12
        xa = np.take_along_axis(x, a.reshape(N, 8, 1, 16 * MA), 3).reshape(N, 8, 16, 16, MA)
        over = xa > np.take_along_axis(lim, jj, 3)[:, :, :, None, :]
        cond = np.add.reduce(over.astype(np.int64), axis=2) >= 9
        ks = np.argmax(np.add.reduce(xa, axis=2), axis=2)[:, :, None]
        b = a + np.take_along_axis(s, a, 3); b = np.where(b >= W, b - W, b)
        n2 = np.take_along_axis(tab, n, 3) >> 12
        a = np.where(cond, b, a); n = np.where(cond, n2, n)
        np.put_along_axis(tab, jj, 4096 * n + a, 3)
        eq = (p & 4095) == a[:, :, :, None]; hit = np.any(eq, axis=3)
        slot = np.where(hit, np.argmax(eq, axis=3), np.argmax(p >> 12, axis=3))[:, :, :, None]
        old = np.take_along_axis(p, slot, 3)[:, :, :, 0]
        send = np.where(hit, p[:, :, :, P - 1], old)
        np.put_along_axis(p, slot, (4096 * n + a)[:, :, :, None], 3)
        p[:, :, :, P - 1] = np.roll(send, 1, axis=0)
        v = np.take_along_axis(np.where(hit, a, old & 4095), ks, 2)[:, :, 0]; up = np.take_along_axis(hit, ks, 2)[:, :, 0]
        j = np.take_along_axis(n, ks, 2)[:, :, 0]
        low = np.full((N, 8, W), MA); np.minimum.at(low, (qa, ga, v), np.arange(MA)[None, None, :])
        wears = np.take_along_axis(up, np.minimum(low, MA - 1), 2)[:, :, None]
        x = np.where((low < MA)[:, :, None], np.where(wears, np.minimum(x + wr[:, :, :, t:t + 1], 255), np.maximum(x - 8, 0)), x)
    return {"yx": x.reshape(N, 128, W).astype(np.float32).astype(BF), "yp": p.reshape(N, 128, P * MA).astype(np.float32)}

@@ -1,0 +1,509 @@
+from concourse.mybir import AluOpType as A, ActivationFunctionType as AF
+
+NT = 3
+TRASH = 1024
+PB = ["p%d" % i for i in range(8)]
+SCRATCH = {p: ("psum", [128, 512], "float32") for p in PB}
+WHERE = {}
+
+
+def _own(name, cols, dtype):
+    SCRATCH[name] = ("sbuf", [128, cols], dtype)
+    WHERE[name] = (name, 0, cols)
+
+
+def _arena(buf, dtype, pieces):
+    c = 0
+    for name, w in pieces:
+        WHERE[name] = (buf, c, w)
+        c += (w + 15) // 16 * 16
+    SCRATCH[buf] = ("sbuf", [128, c], dtype)
+
+
+for _n, _w, _d in (("X", 4096 + TRASH, "bfloat16"), ("D", 4096, "bfloat16"), ("LM", 768, "bfloat16"), ("RT", 3, "bfloat16"), ("JT", 768, "int32"),
+                   ("PK", 384, "int32"), ("JM", 8, "int32"), ("TL", 768, "float32"), ("NX", 768, "float32"), ("IB", 768, "int32"), ("IC", 768, "int32"),
+                   ("ONE", 512, "bfloat16"), ("ZER", 512, "bfloat16"), ("BIG", 512, "bfloat16"), ("TRI", 512, "bfloat16"), ("EYE", 128, "bfloat16"),
+                   ("EYE4", 128, "bfloat16"), ("NEYE", 128, "bfloat16"), ("NEYE8", 128, "bfloat16"), ("G8A", 8, "bfloat16"), ("G8", 8, "bfloat16"),
+                   ("BOA", 128, "bfloat16"), ("BO", 128, "bfloat16"), ("GM", 1024, "bfloat16"), ("GMA", 1024, "bfloat16"), ("NGM", 1024, "bfloat16"),
+                   ("CS", 144, "bfloat16"), ("DI", 2048, "bfloat16"), ("EX", 2048, "bfloat16"), ("RST", 256, "float32"), ("KC", 256, "bfloat16"),
+                   ("GD", 16, "bfloat16"), ("MM", 8, "float32"), ("WI", 256, "float32"), ("WS", 256, "float32"), ("WF", 256, "float32"),
+                   ("RTF", 3, "float32"), ("RT8", 3, "float32"), ("M3", 384, "float32"), ("PF", 384, "int32"), ("PG", 384, "float32"),
+                   ("PM", 384, "int32"), ("YP", 384, "float32")):
+    _own(_n, _w, _d)
+for _t in range(NT):
+    for _n, _w, _d in (("XA", 2048, "bfloat16"), ("OV", 2048, "bfloat16"), ("DG", 2048, "bfloat16"), ("N2", 2048, "float16"), ("GV", 128, "int32"),
+                       ("LAND", 128, "int32")):
+        _own("%s%d" % (_n, _t), _w, _d)
+    SCRATCH["E3%d" % _t] = ("sbuf", [128, 8, 32], "bfloat16")
+    SCRATCH["EE%d" % _t] = ("sbuf", [128, 8, 128], "bfloat16")
+    _arena("u%d" % _t, "uint16", [("%s%d" % (n, _t), w) for n, w in (("JL", 8), ("aL", 128), ("nL", 128), ("VL", 8), ("OF", 8))])
+    _arena("f%d" % _t, "float32", [("%s%d" % (n, _t), w) for n, w in (
+        ("aF", 128), ("pm", 256), ("cS", 128), ("nN", 128), ("U", 128), ("Uc", 128), ("ms", 128), ("ux", 128), ("y1", 128), ("wr", 128), ("ab", 512),
+        ("VF", 8), ("dl", 128), ("xg", 128), ("qn", 128), ("q", 128), ("w", 256), ("OFa", 8), ("OFb", 8))])
+    _arena("i%d" % _t, "int32", [("%s%d" % (n, _t), w) for n, w in (("EQ", 128), ("evM", 128), ("evS", 128), ("M", 384), ("Q", 384))])
+    _arena("b%d" % _t, "bfloat16", [("%s%d" % (n, _t), w) for n, w in (("Lj", 128), ("LT", 128), ("OH", 128), ("e", 384), ("r", 256), ("MW", 128), ("xc", 128),
+                                                                       ("ws", 128))])
+    _arena("h%d" % _t, "float16", [("%s%d" % (n, _t), w) for n, w in (("MN", 128), ("MV", 128), ("nF", 128))])
+_arena("i%d" % NT, "int32", [("Q%d" % NT, 384)])
+SEMAPHORES = ["v", "a", "t", "c"] + ["d%d" % i for i in range(24)] + ["arr%d" % t for t in range(NT)] + ["loc%d" % t for t in range(NT)]
+
+XQ = ("avaa", "aaaa", "vaaa")
+DQ = ("avva", "aaaa", "aaav")
+NQ = ("vaaa", "aavv", "aaaa")
+CQ = ("aa", "vv", "vv")
+EB = ("va", "va", "va")
+ORDER = ("nxd", "dxn", "dxn")
+SEED = 128438
+SPREAD = 0.6
+WAKE = 0.10
+TOL = 0.08
+CYC = 0.83e-3
+PEC = 0.42e-3
+
+
+def build(ops, g, T):
+    n = len(ops)
+    acc = {}
+    chain = {}
+    soft = [None] * n
+    pred = [[] for _ in range(n)]
+    for i, o in enumerate(ops):
+        ps = set()
+        for buf, lo, hi, wr in o["acc"]:
+            psum = buf in PB
+            for j, lo2, hi2, wr2 in acc.setdefault(buf, []):
+                if (lo < hi2 and lo2 < hi and (wr or wr2)) or (psum and ops[j]["q"] != o["q"]):
+                    if not (o.get("grp") and o["grp"] == ops[j].get("grp")):
+                        ps.add(j)
+        for buf, lo, hi, wr in o["acc"]:
+            acc[buf].append((i, lo, hi, wr))
+        ps.discard(i)
+        pred[i] = sorted(ps)
+        o["pred"] = pred[i]
+        k = o.get("line")
+        if k:
+            soft[i] = chain.get(k)
+            chain[k] = i
+    succ = [[] for _ in range(n)]
+    left = [len(p) for p in pred]
+    for i in range(n):
+        for j in pred[i]:
+            succ[j].append(i)
+        if soft[i] is not None and soft[i] not in pred[i]:
+            succ[soft[i]].append(i)
+            left[i] += 1
+    prio = [0.0] * n
+    for i in range(n - 1, -1, -1):
+        prio[i] = ops[i]["cost"] + ops[i]["lat"] + max([prio[s] + WAKE for s in succ[i]] + [0.0])
+    h = SEED
+    for i in range(n):
+        h = (h * 1103515245 + 12345) % 2147483648
+        if ops[i]["kind"] == "load":
+            prio[i] = 1e6 - 1e3 * i
+        else:
+            prio[i] += SPREAD * (h / 2147483648.0)
+    done = [None] * n
+    free = {}
+    link = [0.0]
+    ready = {i for i in range(n) if not left[i]}
+    order = []
+    while ready:
+        best = None
+        ests = {}
+        for i in ready:
+            est = max([free.get(ops[i]["q"], 0.0)] + [done[j] + WAKE for j in pred[i]])
+            ests[i] = est
+            if best is None or est < ests[best] or (est == ests[best] and i < best):
+                best = i
+        q = ops[best]["q"]
+        lim = ests[best] + TOL
+        pick = max((i for i in ready if ops[i]["q"] == q and ests[i] <= lim), key=lambda i: (prio[i], -i))
+        ready.discard(pick)
+        o = ops[pick]
+        st = ests[pick]
+        free[q] = st + o["cost"]
+        if o["kind"] in ("load", "dma"):
+            link[0] = max(link[0], st + 1.3) + o["bytes"] / 250e3
+            done[pick] = link[0] + 0.7
+        else:
+            done[pick] = st + o["cost"] + o["lat"]
+        o["when"] = (st, done[pick])
+        o["pos"] = len(order)
+        order.append(pick)
+        for s in succ[pick]:
+            left[s] -= 1
+            if not left[s]:
+                ready.add(s)
+    eng = {"v": g.vector, "a": g.scalar, "t": g.tensor, "c": g, "s": g.sync}
+    known = {q: {} for q in eng}
+    count = {q: 0 for q in eng}
+    comp = [None] * n
+    clock = [None] * n
+    total = {}
+    nd = 0
+    for i in order:
+        o = ops[i]
+        q = o["q"]
+        if o["kind"] == "arrive":
+            comp[i] = (o["sem"], o["val"])
+            clock[i] = {}
+            total[o["sem"]] = o["val"]
+            continue
+        kn = known[q]
+        need = {}
+        for j in pred[i]:
+            s, v = comp[j]
+            if kn.get(s, 0) < v and need.get(s, (0, 0))[0] < v:
+                need[s] = (v, j)
+        for s in sorted(need, key=lambda s: -need[s][1]):
+            v, j = need[s]
+            if kn.get(s, 0) >= v:
+                continue
+            eng[q].wait_ge(T.sem[s], v)
+            kn[s] = v
+            for s2, v2 in clock[j].items():
+                if kn.get(s2, 0) < v2:
+                    kn[s2] = v2
+        clock[i] = dict(kn)
+        if o["kind"] in ("load", "dma"):
+            s = "d%d" % nd
+            nd += 1
+            o["fns"][0](eng[q]).then_inc(T.sem[s], 16)
+            comp[i] = (s, 16)
+        elif o["kind"] == "remote":
+            o["fns"][0](g)
+            comp[i] = (o["sem"], o["val"])
+        else:
+            for f in o["fns"]:
+                f(eng[q]).then_inc(T.sem[q], 1)
+            count[q] += len(o["fns"])
+            comp[i] = (q, count[q])
+        total[comp[i][0]] = comp[i][1]
+    for s in sorted(total):
+        if known["c"].get(s, 0) < total[s]:
+            g.wait_ge(T.sem[s], total[s])
+    return max(d for d in done if d is not None)
+
+
+def rank_program(g, core, T, topo):
+    rank = T.rank_of(core)
+    if rank is None:
+        return
+    nxt = T.cores[(rank + 1) % len(T.cores)]
+    prv = T.cores[(rank - 1) % len(T.cores)]
+    build(make(core, nxt, prv, T, topo), g, T)
+
+
+def make(core, nxt, prv, T, topo):
+    ops = []
+
+    def norm(x):
+        x = (x,) if isinstance(x, str) else x
+        buf, c0, w = WHERE.get(x[0], (x[0], 0, 512))
+        lo, hi = (x[1], x[2]) if len(x) > 1 else (0, w)
+        return buf, c0 + lo, c0 + hi, (x[3] if len(x) > 3 else 1)
+
+    def ap(x):
+        if isinstance(x, list):
+            return x[0]()
+        buf, lo, hi, st = norm(x)
+        return T[buf][:, lo:hi:st] if st > 1 else T[buf][:, lo:hi]
+
+    def reg(x, wr):
+        if x[:2] in ("E3", "EE"):
+            return (x, 0, 9999, wr)
+        return norm(x)[:3] + (wr,)
+
+    def op(q, fns, R, W, cost, kind="op", lat=0.0, **kw):
+        o = {"q": q, "fns": fns if isinstance(fns, list) else [fns], "acc": [reg(x, False) for x in R] + [reg(x, True) for x in W], "cost": cost,
+             "kind": kind, "lat": lat}
+        o.update(kw)
+        ops.append(o)
+
+    def width(x):
+        _, lo, hi, st = norm(x)
+        return (hi - lo + st - 1) // st
+
+    def isps(x):
+        return (x if isinstance(x, str) else x[0]) in PB
+
+    def vc(c):
+        return 0.05 + max(64, c) * CYC
+
+    def tt(out, a, b, o):
+        op("v", lambda e: e.tensor_tensor(ap(out), ap(a), ap(b), o), [a, b], [out], vc(width(a) * (1 if isps(a) or isps(b) else 2)))
+
+    def ts(out, a, s1, o1, s2=None, o2=None):
+        f = (lambda e: e.tensor_scalar(ap(out), ap(a), s1, None, o1)) if o2 is None else (lambda e: e.tensor_scalar(ap(out), ap(a), s1, s2, o1, o2))
+        op("v", f, [a], [out], vc(width(a)))
+
+    def cp(q, out, a):
+        if q == "v":
+            op("v", lambda e: e.tensor_copy(ap(out), ap(a)), [a], [out], vc(width(a) * 0.5))
+        else:
+            act(out, a, AF.Copy)
+
+    def act(out, a, f, **kw):
+        op("a", lambda e: e.activation(ap(out), ap(a), f, **kw), [a], [out], 0.07 + max(64, width(a)) * CYC)
+
+    def gather(q, out, win, w, lst, line=None):
+        n = 16 * width(lst)
+        if q == "v":
+            op("v", lambda e: e.tensor_copy(ap(out), T[win][:, 0:w].indirect(ap(lst))), [(win, 0, w), lst], [out], 0.05 + n * 1.5 * CYC, line=line and line + q)
+        else:
+            op("a", lambda e: e.activation(ap(out), T[win][:, 0:w].indirect(ap(lst)), AF.Copy), [(win, 0, w), lst], [out], 0.065 + n * 1.5 * CYC,
+               line=line and line + q)
+
+    def scatter(win, w, lst, val):
+        op("v", lambda e: e.tensor_copy(T[win][:, 0:w].indirect(ap(lst)), ap(val)), [lst, val], [(win, 0, w)], 0.05 + 16 * width(lst) * 3 * CYC)
+
+    def mm(out, parts, rd, start=True, stop=True, each=False, grp=None):
+        k = len(parts)
+        fns = [(lambda e, i=i, a=a: e.matmul(ap(a[0]), ap(a[1]), ap(a[2]), each or (start and i == 0), each or (stop and i == k - 1))) for i, a in enumerate(parts)]
+        op("t", fns, list(rd), [out], sum(max(64, width(a[2])) for a in parts) * PEC + 0.01 * k, grp=grp, line=grp)
+
+    def load(dst, src, nbytes, lo=0, hi=None):
+        op("s", lambda e: e.dma_start(ap(dst), T[src][:, lo:hi] if hi else T[src][:]), [], [dst], 0.06, kind="load", bytes=nbytes)
+
+    def fill(x, val):
+        op("v", lambda e: e.memset(ap(x), val), [], [x], vc(width(x) * 0.5))
+
+    def sel(out, a, pat, base, cm, cmp=A.is_ge, other=0.0):
+        op("c", lambda e: e.affine_select(ap(out), ap(a), pat, cmp, other, base, cm), [a], [out], 0.17 + 2 * width(out) * CYC)
+
+    def iota(out, pat, base, cm):
+        op("c", lambda e: e.iota(ap(out), pat, base, cm, allow_small_or_imprecise_dtypes=True), [], [out], 0.13 + 2 * width(out) * CYC)
+
+    load("JM", "jm", 4096)
+    load("JT", "jt", 128 * 768 * 4)
+    load(("D", 3840, 4096), "sd", 64 << 10, 3840, 4096)
+    load("RT", "rt", 768)
+    load("LM", "lm", 128 * 768 * 2)
+    load(("X", 0, 4096), "xw", 1 << 20)
+    load("PK", "pk", 128 * 384 * 4)
+    load(("D", 0, 3840), "sd", 960 << 10, 0, 3840)
+
+    fill("ONE", 1.0)
+    fill("BIG", 8192.0)
+    sel("EYE", ("ONE", 0, 128), [[-1, 128]], 0, 1, A.is_equal)
+    sel("G8A", ("ONE", 0, 8), [[-16, 8]], 0, 1)
+    sel("G8", "G8A", [[16, 8]], 15, -1)
+    sel("BOA", ("ONE", 0, 128), [[-16, 8], [0, 16]], 0, 1)
+    sel("BO", "BOA", [[16, 8], [0, 16]], 15, -1)
+    iota("KC", [[0, 16], [-1, 16]], 15, 0)
+    iota("MM", [[128, 8]], 4096, 1)
+    sel("TRI", "BIG", [[0, 4], [-1, 128]], 0, 1)
+    iota("WI", [[1, 256]], 3840, 0)
+    fill("RST", 1.0)
+    fill(("RST", 0, 256, 32), 0.0)
+    fill("CS", 0.0)
+    cp("v", ("CS", 15, 143, 16), "G8")
+    fill("DI", 0.0)
+    fill("ZER", 0.0)
+    for h in range(4):
+        sel(("EX", 512 * h, 512 * h + 512), "ZER", [[-1, 32], [0, 16]], -32 * h, 1, A.not_equal, 1.0)
+    ts(("GD", 0, 16, 2), "G8", 16.0, A.mult)
+    ts(("GD", 1, 16, 2), "G8", 16.0, A.mult)
+    for k in range(16):
+        cp("a", ("DI", k * 128 + k, k * 128 + 128, 16), ("EYE", k, 128, 16))
+    for h in range(2):
+        x = ("GMA", 512 * h, 512 * h + 512)
+        sel(x, "ONE", [[-16, 4], [0, 128]], -64 * h, 1)
+        sel(("GM", 512 * h, 512 * h + 512), x, [[16, 4], [0, 128]], 64 * h + 15, -1)
+    act("NGM", "GM", AF.Copy, scale=-1.0)
+    act("EYE4", "EYE", AF.Copy, scale=4.0)
+    act("NEYE", "EYE", AF.Copy, scale=-1.0)
+    act("NEYE8", "EYE", AF.Copy, scale=-8.0)
+
+    def CS(k):
+        return ("CS", 15 - k, 143 - k)
+
+    def DI(k):
+        return ("DI", 128 * k, 128 * k + 128)
+
+    cp("v", "JL0", "JM")
+    ts("IC", "JT", 4095, A.bitwise_and)
+    cp("v", "TL", "IC")
+    ts("IB", "JT", 12, A.logical_shift_right)
+    cp("v", "NX", "IB")
+    we = ("D", 3840, 4096)
+    tt("WS", we, "WI", A.add)
+    ts("WF", "WS", 4096.0, A.is_ge, -256.0, A.mult)
+    tt(we, we, "WF", A.add)
+    cp("v", "RTF", "RT")
+    ts("RT8", "RT", -1.0, A.mult, -8.0, A.add)
+    ts("M0", "PK", 4095, A.bitwise_and)
+    ts("M3", "M0", -3.0, A.mult)
+    for i in range(3):
+        ts(("PG", 128 * i, 128 * i + 128), ("PK", 128 * i, 128 * i + 128), 4.0, A.mult, 4096.0 * (2 - i), A.add)
+    tt("Q0", "PG", "M3", A.add)
+
+    for t in range(NT):
+        def n_(x, t=t):
+            return "%s%d" % (x, t)
+        last = t == NT - 1
+        JL, aL, nL, XA, OV, DG, N2 = (n_(x) for x in ("JL", "aL", "nL", "XA", "OV", "DG", "N2"))
+        Q2 = ("Q0", 256, 384) if t == 0 else "LAND%d" % (t - 1)
+        Q0, Q1, Q01 = (n_("Q"), 0, 128), (n_("Q"), 128, 256), (n_("Q"), 0, 256)
+        tA, tB, tC, tD = (("p7", 128 * i, 128 * i + 128) for i in range(4))
+        tCD = ("p7", 256, 512)
+        OHA = ("p4", 256, 384)
+        gather("v", aL, "TL", 768, JL)
+        gather("a", n_("Lj"), "LM", 768, JL)
+        gather("v", nL, "NX", 768, JL)
+        gather("a", n_("aF"), "TL", 768, JL)
+        gather("a", n_("nF"), "NX", 768, JL)
+        o = ("p0", 0, 128)
+        mm(o, [(o, n_("Lj"), "EYE")], [n_("Lj"), "EYE"])
+        cp("a", n_("LT"), o)
+
+        def wear():
+            for q, e in enumerate(XQ[t]):
+                gather(e, (XA, 512 * q, 512 * q + 512), "X", 4096, (aL, 32 * q, 32 * q + 32), "g%d" % t)
+
+        def dist():
+            for q, e in enumerate(DQ[t]):
+                gather(e, (DG, 512 * q, 512 * q + 512), "D", 4096, (aL, 32 * q, 32 * q + 32), "g%d" % t)
+
+        def second():
+            for q, e in enumerate(NQ[t]):
+                gather(e, (N2, 512 * q, 512 * q + 512), "NX", 768, (nL, 32 * q, 32 * q + 32), "g%d" % t)
+        for y in ORDER[t]:
+            {"d": dist, "n": second, "x": wear}[y]()
+        for q in range(4):
+            c, b = (XA, 512 * q, 512 * q + 512), "p%d" % (q // 2)
+            o, x = (OV, 512 * q, 512 * q + 512), ("EX", 512 * q, 512 * q + 512)
+            if CQ[t][q // 2] == "v":
+                mm(b, [(b, n_("LT"), x)], [n_("LT"), x])
+                tt(o, c, b, A.is_gt)
+            else:
+                mm(b, [(b, n_("LT"), x), (b, "NEYE", c)], [n_("LT"), x, "NEYE", c])
+                act(o, b, AF.Sign, scale=-1.0, bias=-0.5)
+        k2 = ("p4", 0, 256)
+        mm(k2, [(k2, "EYE", "KC")], ["EYE", "KC"], stop=False, grp="k%d" % t)
+        mm(k2, [(("p4", k, 256, 16), (XA, k, 2048, 16), "GD") for k in range(16)], [XA, "GD"], start=False, grp="k%d" % t)
+        op("v", lambda e, x=n_("pm"): e.tensor_tensor_scan(ap(x), ap("RST"), ap(("p4", 0, 256)), 0.0, A.mult, A.max), ["RST", k2], [n_("pm")], vc(256))
+        op("v", lambda e, t=t: e.tensor_tensor(T["E3%d" % t][:, :, :], ap(("p4", 0, 256)), ap("pm%d" % t), A.is_equal), [k2, n_("pm")], ["E3%d" % t], vc(256))
+        op("a", lambda e, t=t: e.activation(ap("OH%d" % t), T["E3%d" % t][:, :, 16:32], AF.Copy), ["E3%d" % t], [n_("OH")], 0.18)
+        mm(OHA, [(OHA, n_("OH"), "EYE")], [n_("OH"), "EYE"])
+        for h in range(2):
+            o = ("p5", 64 * h, 64 * h + 64)
+            mm(o, [(o, CS(k), (OV, 1024 * h + k, 1024 * h + 1024, 16)) for k in range(16)], ["CS", (OV, 1024 * h, 1024 * h + 1024)])
+        for h in range(2):
+            ts((n_("cS"), 64 * h, 64 * h + 64), ("p5", 64 * h, 64 * h + 64), 8.5 if CQ[t][h] == "v" else 1.0, A.is_ge)
+
+        def pick_n():
+            for h in range(2):
+                o = ("p2", 64 * h, 64 * h + 64)
+                mm(o, [(o, DI(k), (N2, 1024 * h + k, 1024 * h + 1024, 16)) for k in range(16)] + [(o, "NEYE", (n_("nF"), 64 * h, 64 * h + 64))],
+                   ["DI", (N2, 1024 * h, 1024 * h + 1024), "NEYE", n_("nF")])
+
+        def pick_d():
+            for h in range(2):
+                o = ("p6", 64 * h, 64 * h + 64)
+                mm(o, [(o, DI(k), (DG, 1024 * h + k, 1024 * h + 1024, 16)) for k in range(16)], ["DI", (DG, 1024 * h, 1024 * h + 1024)])
+        for f in ((pick_n, pick_d) if t == 0 else (pick_d, pick_n)):
+            f()
+        act(n_("ws"), ("p6", 0, 128), AF.Sign, bias=0.5)
+        act(n_("wr"), n_("ws"), AF.Copy, scale=1920.0, bias=-1920.0)
+        tt(tC, ("p6", 0, 128), n_("wr"), A.add)
+        tt(tA, n_("cS"), ("p2", 0, 128), A.mult)
+        tt(n_("nN"), tA, n_("nF"), A.add)
+        if not last:
+            tt(n_("MN"), n_("nN"), OHA, A.mult)
+            mm(("p4", 0, 8), [(("p4", 0, 8), CS(k), (n_("MN"), k, 128, 16)) for k in range(16)], ["CS", n_("MN")])
+            cp("v", "JL%d" % (t + 1), ("p4", 0, 8))
+            scatter("NX", 768, JL, n_("nN"))
+        tt(tC, n_("cS"), tC, A.mult)
+        tt(tB, tC, n_("aF"), A.add)
+        tt(n_("U"), tC, n_("aF"), A.add)
+        act(n_("Uc"), n_("U"), AF.Identity, bias=-2048.0)
+        if not last:
+            scatter("TL", 768, JL, n_("U"))
+        if t:
+            ts((n_("M"), 256, 384), Q2, 4095, A.bitwise_and)
+        tt(tD, Q0, Q1, A.max)
+        tt(n_("EQ"), tD, Q2, A.max)
+        r0, r1 = (n_("r"), 0, 128), (n_("r"), 128, 256)
+        tt(r0, Q0, n_("EQ"), A.is_equal)
+        tt(r1, Q1, n_("EQ"), A.is_equal)
+        ts(n_("evM"), n_("EQ"), 4095, A.bitwise_and)
+        ts(n_("evS"), n_("EQ"), 0xFFCFFF, A.bitwise_and)
+        tt(tD, n_("evS"), Q2, A.subtract)
+        e0, e1, e2 = ((n_("e"), 128 * i, 128 * i + 128) for i in range(3))
+        for i, x in enumerate((e0, e1, e2)):
+            tt(x, (n_("M"), 128 * i, 128 * i + 128), tB, A.is_equal)
+        o = ("p5", 128, 256)
+        mm(o, [(o, "EYE", e0), (o, "EYE", e1), (o, "EYE", e2)], ["EYE", n_("e")])
+        act(n_("ms"), o, AF.Relu, scale=-1.0, bias=1.0)
+        tt(n_("ux"), n_("evM"), tB, A.subtract)
+        tt(tC, n_("ux"), OHA, A.mult)
+        tt(n_("y1"), n_("Uc"), OHA, A.mult)
+        tt(tC, n_("ms"), tC, A.mult)
+        tt(n_("MV"), tC, n_("y1"), A.add)
+        tt(n_("MW"), n_("ms"), OHA, A.mult)
+        for b in range(2):
+            o = "p%d" % (2 + b)
+            mm(o, [(o, "EYE", "TRI")], ["EYE", "TRI"], stop=False, grp="e%d%d" % (t, b))
+            mm(o, [(o, n_("MV"), ("NGM", 512 * b, 512 * b + 512))] +
+               [((o, 128 * x, 128 * x + 128), ("GM", 128 * (4 * b + x), 128 * (4 * b + x) + 128), n_("MV")) for x in range(4)],
+               [n_("MV"), "NGM", "GM"], start=False, grp="e%d%d" % (t, b))
+        o = ("p4", 8, 16)
+        mm(o, [(o, CS(k), (n_("MV"), k, 128, 16)) for k in range(16)], ["CS", n_("MV")])
+        ts(n_("VL"), o, 2048.0, A.add)
+        act(n_("VF"), o, AF.Identity, bias=2048.0)
+        o = ("p1", 0, 128)
+        mm(o, [(o, "BO", n_("MW"))], ["BO", n_("MW")])
+        op("a", lambda e, t=t: e.activation(ap("dl%d" % t), ap(("p1", 0, 128)), AF.Identity, bias=ap(("RTF", t, t + 1)), scale=ap(("RT8", t, t + 1))),
+           [o, "RTF", "RT8"], [n_("dl")], 0.18)
+        for x in range(8):
+            o = ("p%d" % (2 + x // 4), 128 * (x % 4), 128 * (x % 4) + 128)
+            if EB[t][x // 4] == "v":
+                op("v", lambda e, x=x, t=t, o=o: e.tensor_scalar(T["EE%d" % t][:, :, 16 * x:16 * x + 16], ap(o), 0.0, None, A.is_equal), [o], [], 0.16)
+            else:
+                if x % 4 == 0:
+                    act(n_("ab"), "p%d" % (2 + x // 4), AF.Abs)
+                o = (n_("ab"), 128 * (x % 4), 128 * (x % 4) + 128)
+                op("a", lambda e, x=x, t=t, o=o: e.activation(T["EE%d" % t][:, :, 16 * x:16 * x + 16], ap(o), AF.Relu, scale=-1.0, bias=1.0), [o], [], 0.18)
+            ops[-1]["acc"].append(("EE%d" % t, x, x + 1, True))
+        op("v", lambda e, t=t: e.tensor_tensor(ap("xg%d" % t), T.X[:, 0:4096].indirect(ap("VL%d" % t)), ap("dl%d" % t), A.add),
+           [("X", 0, 4096), n_("VL"), n_("dl")], [n_("xg")], 0.22)
+        ts(n_("xc"), n_("xg"), 0.0, A.max, 255.0, A.min)
+        o = ("p4", 16, 24)
+        mm(o, [(("p4", 16 + c, 17 + c), [lambda c=c, t=t: T["EE%d" % t][:, c, :]], ("BIG", 0, 1)) for c in range(8)], ["EE%d" % t, "BIG"], each=True)
+        tt(n_("OFa"), o, "MM", A.min)
+        tt(n_("OFb"), n_("OFa"), n_("VF"), A.max)
+        cp("v", n_("OF"), n_("OFb"))
+        scatter("X", 4096 + TRASH, n_("OF"), n_("xc"))
+        tt(tD, n_("ms"), tD, A.mult)
+        tt(n_("GV"), tD, Q2, A.add)
+        out = topo.engines(core, nxt)[:8]
+        rin = topo.engines(prv, core)[:8]
+        rid, pid = topo.addr(nxt)[:2]
+        op("c", lambda e, t=t, rid=rid, pid=pid, m=sum(1 << x for x in out): e.remote_dma(
+            T["LAND%d" % t][:], T["GV%d" % t][:], T.sem["arr%d" % t], T.sem["loc%d" % t], pid, rid, m),
+           [n_("GV")], [("SENT%d" % t, 0, 1)], 0.3, kind="remote", lat=2.0, sem="loc%d" % t, val=len(out))
+        op("z%d" % t, None, [("SENT%d" % t, 0, 1)], ["LAND%d" % t], 0.0, kind="arrive", lat=2.0, sem="arr%d" % t, val=len(rin))
+        act(n_("qn"), n_("nN"), AF.Copy, scale=16384.0)
+        tt(n_("q"), n_("qn"), tB, A.add)
+        act(("p3", 0, 128), n_("q"), AF.Identity, bias=8192.0)
+        act(("p3", 128, 256), n_("q"), AF.Identity, bias=4096.0)
+        o = ("p5", 256, 384)
+        mm(o, [(o, "EYE4", e0), (o, "NEYE", e1), (o, "NEYE", e2), (o, "EYE", r0)], ["EYE4", "NEYE", "EYE", n_("e"), n_("r")])
+        o = ("p5", 384, 512)
+        mm(o, [(o, "NEYE8", e0), (o, "EYE4", e1), (o, "NEYE", e2), (o, "EYE", r1)], ["EYE4", "NEYE8", "NEYE", "EYE", n_("e"), n_("r")])
+        ts(n_("w"), ("p5", 256, 512), 0.5, A.is_ge)
+        tt(tCD, ("p3", 0, 256), Q01, A.subtract)
+        tt(tCD, n_("w"), tCD, A.mult)
+        tt(("Q%d" % (t + 1), 0, 256), tCD, Q01, A.add)
+        if not last:
+            ts(("M%d" % (t + 1), 0, 256), ("Q%d" % (t + 1), 0, 256), 4095, A.bitwise_and)
+
+    for src, lo, hi in ((("Q%d" % NT, 0, 256), 0, 256), ("LAND%d" % (NT - 1), 256, 384)):
+        ts(("PF", lo, hi), src, 0xFFC000, A.bitwise_and)
+        ts(("PM", lo, hi), src, 4095, A.bitwise_and)
+        ts(("PG", lo, hi), ("PF", lo, hi), 0.25, A.mult)
+        tt(("YP", lo, hi), ("PG", lo, hi), ("PM", lo, hi), A.add)
+    op("s", lambda e: e.dma_start(T.yx[:], ap(("X", 0, 4096))), [("X", 0, 4096)], [("OUTX", 0, 1)], 0.06, kind="dma", bytes=1 << 20, lat=7.0)
+    op("s", lambda e: e.dma_start(T.yp[:], ap("YP")), ["YP"], [("OUTP", 0, 1)], 0.06, kind="dma", bytes=128 * 384 * 4, lat=3.0)
+    return ops

@@ -1,9 +1,9 @@
 from concourse.mybir import AluOpType as A, ActivationFunctionType as AF
 
 NT = 3
-TRASH = 1024
+TRASH = 256
 PB = ["p%d" % i for i in range(8)]
-SCRATCH = {p: ("psum", [128, 512], "float32") for p in PB}
+SCRATCH = {p: ("psum", [128, 4, 128] if p in ("p2", "p3") else [128, 512], "float32") for p in PB}
 WHERE = {}
 
 
@@ -20,45 +20,235 @@ def _arena(buf, dtype, pieces):
     SCRATCH[buf] = ("sbuf", [128, c], dtype)
 
 
+EYES = {"NEYE": -1.0, "N2": -2.0, "E8": 8.0, "N16": -16.0, "E1K": 1024.0, "N2K": -2048.0, "E4K": 4096.0, "E12K": 12288.0, "N12K": -12288.0,
+        "E16K": 16384.0, "N16K": -16384.0, "N16M": -2.0 ** 24, "E32M": 2.0 ** 25}
 for _n, _w, _d in (("X", 4096 + TRASH, "bfloat16"), ("D", 4096, "bfloat16"), ("LM", 768, "bfloat16"), ("RT", 3, "bfloat16"), ("JT", 768, "int32"),
-                   ("PK", 384, "int32"), ("JM", 8, "int32"), ("TL", 768, "float32"), ("NX", 768, "float32"), ("IB", 768, "int32"), ("IC", 768, "int32"),
-                   ("ONE", 512, "bfloat16"), ("ZER", 512, "bfloat16"), ("BIG", 512, "bfloat16"), ("TRI", 512, "bfloat16"), ("EYE", 128, "bfloat16"),
-                   ("EYE4", 128, "bfloat16"), ("NEYE", 128, "bfloat16"), ("NEYE8", 128, "bfloat16"), ("G8A", 8, "bfloat16"), ("G8", 8, "bfloat16"),
-                   ("BOA", 128, "bfloat16"), ("BO", 128, "bfloat16"), ("GM", 1024, "bfloat16"), ("GMA", 1024, "bfloat16"), ("NGM", 1024, "bfloat16"),
-                   ("CS", 144, "bfloat16"), ("DI", 2048, "bfloat16"), ("EX", 2048, "bfloat16"), ("RST", 256, "float32"), ("KC", 256, "bfloat16"),
-                   ("GD", 16, "bfloat16"), ("MM", 8, "float32"), ("WI", 256, "float32"), ("WS", 256, "float32"), ("WF", 256, "float32"),
-                   ("RTF", 3, "float32"), ("RT8", 3, "float32"), ("M3", 384, "float32"), ("PF", 384, "int32"), ("PG", 384, "float32"),
-                   ("PM", 384, "int32"), ("YP", 384, "float32")):
+                   ("PK", 384, "int32"), ("JM", 8, "int32"), ("JF", 768, "float32"), ("TL", 768, "int32"), ("PKF", 384, "float32"), ("F0", 384, "float16"), ("YP", 384, "float32")):
     _own(_n, _w, _d)
+_arena("cb", "bfloat16", [("ONE", 128), ("MONE", 128), ("ZER", 512), ("BIG", 16), ("TRI", 1024), ("EYE", 128), ("G8A", 8), ("G8", 8), ("BOA", 128), ("BO", 512),
+                          ("NGM", 1024), ("CS", 144), ("KC", 128), ("KG", 128), ("GD", 8), ("CQ", 384), ("CP", 384), ("CU", 384), ("RST", 128)] + [(n, 128) for n in EYES])
+_arena("cf", "float32", [("EYE32", 128), ("NEYE32", 128), ("PM", 144), ("PN", 128), ("MM", 8), ("RTF", 3), ("RT8", 3)])
 for _t in range(NT):
-    for _n, _w, _d in (("XA", 2048, "bfloat16"), ("OV", 2048, "bfloat16"), ("DG", 2048, "bfloat16"), ("N2", 2048, "float16"), ("GV", 128, "int32"),
-                       ("LAND", 128, "int32")):
+    for _n, _w, _d in (("XA", 2048, "bfloat16"), ("OV", 2048, "bfloat16"), ("DG", 2048, "bfloat16"), ("N2", 2048, "float16"), ("GV", 128, "float32")):
         _own("%s%d" % (_n, _t), _w, _d)
-    SCRATCH["E3%d" % _t] = ("sbuf", [128, 8, 32], "bfloat16")
-    SCRATCH["EE%d" % _t] = ("sbuf", [128, 8, 128], "bfloat16")
+    _own("EE%d" % _t, 1024, "bfloat16")
     _arena("u%d" % _t, "uint16", [("%s%d" % (n, _t), w) for n, w in (("JL", 8), ("aL", 128), ("nL", 128), ("VL", 8), ("OF", 8))])
-    _arena("f%d" % _t, "float32", [("%s%d" % (n, _t), w) for n, w in (
-        ("aF", 128), ("pm", 256), ("cS", 128), ("nN", 128), ("U", 128), ("Uc", 128), ("ms", 128), ("ux", 128), ("y1", 128), ("wr", 128), ("ab", 512),
-        ("VF", 8), ("dl", 128), ("xg", 128), ("qn", 128), ("q", 128), ("w", 256), ("OFa", 8), ("OFb", 8))])
-    _arena("i%d" % _t, "int32", [("%s%d" % (n, _t), w) for n, w in (("EQ", 128), ("evM", 128), ("evS", 128), ("M", 384), ("Q", 384))])
-    _arena("b%d" % _t, "bfloat16", [("%s%d" % (n, _t), w) for n, w in (("Lj", 128), ("LT", 128), ("OH", 128), ("e", 384), ("r", 256), ("MW", 128), ("xc", 128),
-                                                                       ("ws", 128))])
-    _arena("h%d" % _t, "float16", [("%s%d" % (n, _t), w) for n, w in (("MN", 128), ("MV", 128), ("nF", 128))])
-_arena("i%d" % NT, "int32", [("Q%d" % NT, 384)])
+    _arena("f%d" % _t, "float32", [("%s%d" % (n, _t), w) for n, w in (("cS", 128), ("t1", 128), ("EQ", 128), ("tv", 128), ("g1", 128), ("ab", 512), ("rec", 128), ("un", 128),
+                                                                       ("OFa", 8))])
+    _arena("i%d" % _t, "int32", [("%s%d" % (n, _t), w) for n, w in (("rI", 128), ("aI", 128))])
+    _arena("b%d" % _t, "bfloat16", [("%s%d" % (n, _t), w) for n, w in (("Lj", 128), ("OH", 128), ("OHN", 128), ("e", 384), ("sg", 256), ("mw", 128), ("w", 256), ("xc", 128),
+                                                                       ("ws", 128), ("dl", 128))])
+    _arena("h%d" % _t, "float16", [("%s%d" % (n, _t), w) for n, w in (("MN", 128), ("MV", 128), ("nF", 128), ("aH", 128), ("uc", 128), ("t2", 128), ("Fe", 128),
+                                                                      ("xg", 128), ("vc", 128), ("VH", 8))])
+for _t in range(NT + 1):
+    _own("Q%d" % _t, 384, "float32")
+    _own("Fh%d" % _t, 384, "float16")
 SEMAPHORES = ["v", "a", "t", "c"] + ["d%d" % i for i in range(24)] + ["arr%d" % t for t in range(NT)] + ["loc%d" % t for t in range(NT)]
 
-XQ = ("avaa", "aaaa", "vaaa")
-DQ = ("avva", "aaaa", "aaav")
-NQ = ("vaaa", "aavv", "aaaa")
-CQ = ("aa", "vv", "vv")
-EB = ("va", "va", "va")
-ORDER = ("nxd", "dxn", "dxn")
-SEED = 128438
-SPREAD = 0.6
-WAKE = 0.10
-TOL = 0.08
+K = {"XQ": ("avav", "vvaa", "vvaa"), "DQ": ("avav", "aaaa", "aaaa"), "NQ": ("vava", "aaaa", "aaaa"), "CQ": ("vvvv", "vvva", "vvva"), "EB": ("vv", "vv", "vv"),
+     "CUT": 0.2, "WQ": "aaa", "VH": "a", "SL": ("p6", 384), "EO": (0, 1), "ORDER": ("nxd", "ndx", "dxn"), "SEED": 1, "TOL": 0.08, "MOVES": 250000, "HEAT": 0.4, "PULL": 0.003,
+     "WEIGHT": (1.0, 0.5), "LOADS": ("JM", "JT", "X", "LM", "PK", "RT", "D")}
 CYC = 0.83e-3
 PEC = 0.42e-3
+GUESS = ((1.0, 1.56, 3.8, 0.10, 0.05, 250e3), (1.3, 1.3, 5.0, 0.2, 0.1, 300e3), (1.0, 1.2, 2.5, 0.06, 0.03, 350e3))
+PLAN = {}
+
+
+def plan(ops, pred, soft):
+    n = len(ops)
+    succ = [[] for _ in range(n)]
+    left0 = [len(p) for p in pred]
+    for i in range(n):
+        for j in pred[i]:
+            succ[j].append(i)
+        if soft[i] is not None and soft[i] not in pred[i]:
+            succ[soft[i]].append(i)
+            left0[i] += 1
+    isdma = [o["kind"] in ("load", "dma") for o in ops]
+    lat = [o["lat"] for o in ops]
+    cost = [[(o["fix"] + o["cyc"] * {"g": m[1], "s": m[2]}.get(o["per"], 1.0)) * (1.0 if o["kind"] != "op" else m[0]) for o in ops] for m in GUESS]
+    flex = [bool(o.get("alt")) for o in ops]
+
+    def finish(i, st, m, link):
+        if isdma[i]:
+            link[0] = max(link[0], st + 1.5) + ops[i]["bytes"] / GUESS[m][5]
+            return link[0] + 0.5
+        return st + cost[m][i] + lat[i]
+
+    def schedule(prio, qs):
+        w, ws = GUESS[0][3:5]
+        left = list(left0)
+        done = [0.0] * n
+        at = [0.0] * n
+        free = {q: 0.0 for q in qs}
+        ready = {q: [] for q in qs}
+        for i in range(n):
+            if not left[i]:
+                ready[qs[i]].append(i)
+        link = [0.0]
+        order = []
+        tol = K["TOL"]
+        while len(order) < n:
+            est, q = min((max(free[q], min([at[i] for i in r])), q) for q, r in ready.items() if r)
+            lim = est + tol
+            pick = max([i for i in ready[q] if at[i] <= lim], key=lambda i: prio[i])
+            ready[q].remove(pick)
+            st = max(free[q], at[pick])
+            free[q] = st + cost[0][pick]
+            done[pick] = finish(pick, st, 0, link)
+            order.append(pick)
+            for s in succ[pick]:
+                left[s] -= 1
+                if not left[s]:
+                    at[s] = max([done[j] + (ws if qs[j] == qs[s] else w) for j in pred[s]] + [0.0])
+                    ready[qs[s]].append(s)
+        return order, max(done)
+
+    names = sorted({o["q"] for o in ops})
+    outs = [k for k in range(n) if ops[k]["kind"] == "dma"]
+
+    def replay(order, qs, m, a=0, prev=None):
+        w, ws, rate = GUESS[m][3:6]
+        c = cost[m]
+        free = dict.fromkeys(names, 0.0)
+        last = dict.fromkeys(names, -1)
+        link = 0.0
+        if a:
+            done, why = list(prev[1]), list(prev[2])
+            left = 4
+            for i in reversed(order[:a]):
+                q = qs[i]
+                if last[q] < 0:
+                    last[q] = i
+                    free[q] = done[i] - lat[i]
+                    if isdma[i]:
+                        link = done[i] - 0.5
+                        free[q] = 1.0
+                    if q in "vatc":
+                        left -= 1
+                        if not left and link:
+                            break
+        else:
+            done = [0.0] * n
+            why = [-1] * n
+        for i in order[a:]:
+            q = qs[i]
+            st = free[q]
+            y = last[q]
+            for j in pred[i]:
+                d = done[j] + (ws if qs[j] == q else w)
+                if d > st:
+                    st = d
+                    y = j
+            why[i] = y
+            last[q] = i
+            free[q] = e = st + c[i]
+            if isdma[i]:
+                link = max(link, st + 1.5) + ops[i]["bytes"] / rate
+                done[i] = link + 0.5
+            else:
+                done[i] = e + lat[i]
+        return max([done[k] for k in outs]) + K["PULL"] * sum(done), done, why
+
+    prio = [0.0] * n
+    after = {}
+    for i in range(n - 1, -1, -1):
+        prio[i] = cost[0][i] + lat[i] + ops[i].get("tail", 0.0) + max([prio[s] + GUESS[0][3] for s in succ[i]] + [0.0])
+        if ops[i].get("alt") and ops[i]["cyc"] > 0.3:
+            prio[i] = max(prio[i], cost[0][i] + after.get(ops[i]["q"], 0.0))
+            after[ops[i]["q"]] = prio[i]
+    for i in range(n):
+        if ops[i]["kind"] == "load":
+            prio[i] = 1e6 - 1e3 * i
+    qs = [o["q"] for o in ops]
+    order = schedule(prio, qs)[0]
+    h = [K["SEED"]]
+
+    def rnd():
+        h[0] = (h[0] * 1103515245 + 12345) % 2147483648
+        return h[0] / 2147483648.0
+    allp = [pred[i] + ([soft[i]] if soft[i] is not None and soft[i] not in pred[i] else []) for i in range(n)]
+    fixed = [o["kind"] in ("load", "arrive") for o in ops]
+    other = {"a": "v", "v": "a"}
+    W = K["WEIGHT"]
+    M = range(len(W))
+    cur = [replay(order, qs, m) for m in M]
+    cv = sum(W[m] * cur[m][0] for m in M)
+    best = (cv, order, qs)
+    stale = True
+    for it in range(K["MOVES"]):
+        if stale:
+            path = []
+            for m in M:
+                for i in outs:
+                    while i >= 0:
+                        path.append(i)
+                        i = cur[m][2][i]
+            pos = [0] * n
+            for p, i in enumerate(order):
+                pos[i] = p
+            stale = False
+        j = path[int(rnd() * len(path))] if rnd() < 0.6 else int(rnd() * n)
+        if fixed[j]:
+            continue
+        q2, o2, a, b, x = qs, order, pos[j], pos[j], rnd()
+        if flex[j] and x < 0.4:
+            q2 = list(qs)
+            q2[j] = other[qs[j]]
+            near = [k for k in order[max(0, b - 40):b + 40] if flex[k] and qs[k] == q2[j]] if x < 0.2 else []
+            if near:
+                k = near[int(rnd() * len(near))]
+                q2[k] = qs[j]
+                a = min(a, pos[k])
+        elif x > 0.85:
+            lo = max([pos[k] for k in allp[j]] + [-1]) + 1
+            p = lo + int(rnd() * (min([pos[k] for k in succ[j]] + [n]) - lo))
+            if p == b:
+                continue
+            o2 = order[:p] + [j] + order[p:b] + order[b + 1:] if p < b else order[:b] + order[b + 1:p + 1] + [j] + order[p + 1:]
+            a = min(p, b)
+            if flex[j] and rnd() < 0.5:
+                q2 = list(qs)
+                q2[j] = other[qs[j]]
+        else:
+            same = [k for k in order[max(0, b - 60):b] if qs[k] == qs[j]]
+            if not same:
+                continue
+            i = same[-1 - int(min(len(same), 6) * rnd() ** 2)]
+            if fixed[i]:
+                continue
+            a = pos[i]
+            seg = order[a:b + 1]
+            if rnd() < 0.5:
+                up = {j}
+                for k in reversed(seg):
+                    if k in up:
+                        up.update(allp[k])
+                if i in up:
+                    continue
+            else:
+                dn = {i}
+                for k in seg:
+                    if k in dn:
+                        dn.update(succ[k])
+                if j in dn:
+                    continue
+                up = {k for k in seg if k not in dn}
+            o2 = order[:a] + [k for k in seg if k in up] + [k for k in seg if k not in up] + order[b + 1:]
+        if a < 20:
+            a = 0
+        lim = cv + K["HEAT"] * (1.0 - it / K["MOVES"]) * rnd() ** 2
+        new = [replay(o2, q2, 0, a, cur[0])]
+        if W[0] * (new[0][0] - cur[0][0]) > lim - cv + 0.3:
+            continue
+        new += [replay(o2, q2, m, a, cur[m]) for m in M[1:]]
+        v = sum(W[m] * new[m][0] for m in M)
+        if v <= lim:
+            cur, cv, order, qs = new, v, o2, q2
+            stale = True
+            if v < best[0]:
+                best = (v, order, qs)
+    return best[1], best[2], [max(replay(best[1], best[2], m)[1]) for m in range(len(GUESS))]
 
 
 def build(ops, g, T):
@@ -84,56 +274,20 @@ def build(ops, g, T):
         if k:
             soft[i] = chain.get(k)
             chain[k] = i
-    succ = [[] for _ in range(n)]
-    left = [len(p) for p in pred]
-    for i in range(n):
-        for j in pred[i]:
-            succ[j].append(i)
-        if soft[i] is not None and soft[i] not in pred[i]:
-            succ[soft[i]].append(i)
-            left[i] += 1
-    prio = [0.0] * n
-    for i in range(n - 1, -1, -1):
-        prio[i] = ops[i]["cost"] + ops[i]["lat"] + max([prio[s] + WAKE for s in succ[i]] + [0.0])
-    h = SEED
-    for i in range(n):
-        h = (h * 1103515245 + 12345) % 2147483648
-        if ops[i]["kind"] == "load":
-            prio[i] = 1e6 - 1e3 * i
-        else:
-            prio[i] += SPREAD * (h / 2147483648.0)
-    done = [None] * n
-    free = {}
-    link = [0.0]
-    ready = {i for i in range(n) if not left[i]}
-    order = []
-    while ready:
-        best = None
-        ests = {}
-        for i in ready:
-            est = max([free.get(ops[i]["q"], 0.0)] + [done[j] + WAKE for j in pred[i]])
-            ests[i] = est
-            if best is None or est < ests[best] or (est == ests[best] and i < best):
-                best = i
-        q = ops[best]["q"]
-        lim = ests[best] + TOL
-        pick = max((i for i in ready if ops[i]["q"] == q and ests[i] <= lim), key=lambda i: (prio[i], -i))
-        ready.discard(pick)
-        o = ops[pick]
-        st = ests[pick]
-        free[q] = st + o["cost"]
-        if o["kind"] in ("load", "dma"):
-            link[0] = max(link[0], st + 1.3) + o["bytes"] / 250e3
-            done[pick] = link[0] + 0.7
-        else:
-            done[pick] = st + o["cost"] + o["lat"]
-        o["when"] = (st, done[pick])
-        o["pos"] = len(order)
-        order.append(pick)
-        for s in succ[pick]:
-            left[s] -= 1
-            if not left[s]:
-                ready.add(s)
+    if "order" not in PLAN:
+        lean = []
+        above = []
+        for i in range(n):
+            up = set()
+            for j in pred[i]:
+                up |= above[j]
+            lean.append([j for j in pred[i] if j not in up])
+            above.append(up | set(pred[i]))
+        PLAN["order"], PLAN["queue"], PLAN["time"] = plan(ops, lean, soft)
+    order = PLAN["order"]
+    for o, q in zip(ops, PLAN["queue"]):
+        if q != o["q"]:
+            o["q"], o["fns"] = q, o["alt"]
     eng = {"v": g.vector, "a": g.scalar, "t": g.tensor, "c": g, "s": g.sync}
     known = {q: {} for q in eng}
     count = {q: 0 for q in eng}
@@ -182,7 +336,6 @@ def build(ops, g, T):
     for s in sorted(total):
         if known["c"].get(s, 0) < total[s]:
             g.wait_ge(T.sem[s], total[s])
-    return max(d for d in done if d is not None)
 
 
 def rank_program(g, core, T, topo):
@@ -207,25 +360,36 @@ def make(core, nxt, prv, T, topo):
         if isinstance(x, list):
             return x[0]()
         buf, lo, hi, st = norm(x)
+        if len(SCRATCH[buf][1]) == 3:
+            return T[buf][:, lo // 128:hi // 128, :] if hi - lo > 128 else T[buf][:, lo // 128, lo % 128:(hi - 1) % 128 + 1:st]
         return T[buf][:, lo:hi:st] if st > 1 else T[buf][:, lo:hi]
 
     def reg(x, wr):
-        if x[:2] in ("E3", "EE"):
-            return (x, 0, 9999, wr)
+        if isinstance(x, list):
+            return x[1] + (wr,)
         return norm(x)[:3] + (wr,)
 
-    def op(q, fns, R, W, cost, kind="op", lat=0.0, **kw):
-        o = {"q": q, "fns": fns if isinstance(fns, list) else [fns], "acc": [reg(x, False) for x in R] + [reg(x, True) for x in W], "cost": cost,
+    def op(q, fns, R, W, cost, kind="op", lat=0.0, per="", **kw):
+        fix, cyc = cost if isinstance(cost, tuple) else (cost, 0.0)
+        o = {"q": q, "fns": fns if isinstance(fns, list) else [fns], "acc": [reg(x, False) for x in R] + [reg(x, True) for x in W], "fix": fix, "cyc": cyc, "per": per,
              "kind": kind, "lat": lat}
         o.update(kw)
         ops.append(o)
 
     def width(x):
+        if isinstance(x, list):
+            return x[2]
         _, lo, hi, st = norm(x)
         return (hi - lo + st - 1) // st
 
+    def bufof(x):
+        return x[1][0] if isinstance(x, list) else norm(x)[0]
+
     def isps(x):
-        return (x if isinstance(x, str) else x[0]) in PB
+        return bufof(x) in PB
+
+    def two(x):
+        return SCRATCH[bufof(x).split(".")[0]][2] in ("bfloat16", "float16", "uint16")
 
     def vc(c):
         return 0.05 + max(64, c) * CYC
@@ -234,39 +398,48 @@ def make(core, nxt, prv, T, topo):
         op("v", lambda e: e.tensor_tensor(ap(out), ap(a), ap(b), o), [a, b], [out], vc(width(a) * (1 if isps(a) or isps(b) else 2)))
 
     def ts(out, a, s1, o1, s2=None, o2=None):
-        f = (lambda e: e.tensor_scalar(ap(out), ap(a), s1, None, o1)) if o2 is None else (lambda e: e.tensor_scalar(ap(out), ap(a), s1, s2, o1, o2))
-        op("v", f, [a], [out], vc(width(a)))
+        c1 = (lambda: s1) if isinstance(s1, (int, float)) else (lambda: ap(s1))
+        f = (lambda e: e.tensor_scalar(ap(out), ap(a), c1(), None, o1)) if o2 is None else (lambda e: e.tensor_scalar(ap(out), ap(a), c1(), s2, o1, o2))
+        op("v", f, [a] + ([] if isinstance(s1, (int, float)) else [s1]), [out], vc(width(a) * (0.5 if two(a) and two(out) else 1)))
 
     def cp(q, out, a):
         if q == "v":
-            op("v", lambda e: e.tensor_copy(ap(out), ap(a)), [a], [out], vc(width(a) * 0.5))
+            op("v", lambda e: e.tensor_copy(ap(out), ap(a)), [a], [out], vc(width(a) * (0.5 if two(a) and two(out) else 1)))
         else:
             act(out, a, AF.Copy)
 
     def act(out, a, f, **kw):
-        op("a", lambda e: e.activation(ap(out), ap(a), f, **kw), [a], [out], 0.07 + max(64, width(a)) * CYC)
+        op("a", lambda e: e.activation(ap(out), ap(a), f, **kw), [a], [out], 0.065 + max(64, width(a)) * CYC)
 
-    def gather(q, out, win, w, lst, line=None):
+    def gather(q, out, win, w, lst, line=None, mul=None, add=None):
         n = 16 * width(lst)
-        if q == "v":
-            op("v", lambda e: e.tensor_copy(ap(out), T[win][:, 0:w].indirect(ap(lst))), [(win, 0, w), lst], [out], 0.05 + n * 1.5 * CYC, line=line and line + q)
+        fa = lambda e: e.activation(ap(out), T[win][:, 0:w].indirect(ap(lst)), AF.Copy, scale=mul or 1.0, bias=add or 0.0)
+        if mul:
+            f = lambda e: e.tensor_scalar(ap(out), T[win][:, 0:w].indirect(ap(lst)), mul, add, A.mult, A.add)
         else:
-            op("a", lambda e: e.activation(ap(out), T[win][:, 0:w].indirect(ap(lst)), AF.Copy), [(win, 0, w), lst], [out], 0.065 + n * 1.5 * CYC,
-               line=line and line + q)
+            f = lambda e: e.tensor_copy(ap(out), T[win][:, 0:w].indirect(ap(lst)))
+        op(q, fa if q == "a" else f, [(win, 0, w), lst], [out], (0.06, n * CYC), per="g", alt=line and [f if q == "a" else fa])
 
     def scatter(win, w, lst, val):
-        op("v", lambda e: e.tensor_copy(T[win][:, 0:w].indirect(ap(lst)), ap(val)), [lst, val], [(win, 0, w)], 0.05 + 16 * width(lst) * 3 * CYC)
+        op("v", lambda e: e.tensor_copy(T[win][:, 0:w].indirect(ap(lst)), ap(val)), [lst, val], [(win, 0, w)], (0.05, 16 * width(lst) * CYC), per="s")
 
-    def mm(out, parts, rd, start=True, stop=True, each=False, grp=None):
+    def mm(out, parts, start=True, stop=True, each=False, grp=None):
         k = len(parts)
         fns = [(lambda e, i=i, a=a: e.matmul(ap(a[0]), ap(a[1]), ap(a[2]), each or (start and i == 0), each or (stop and i == k - 1))) for i, a in enumerate(parts)]
-        op("t", fns, list(rd), [out], sum(max(64, width(a[2])) for a in parts) * PEC + 0.01 * k, grp=grp, line=grp)
+        grp = grp or "g%d" % len(ops)
+        lo, cost = 0, 0.0
+        for i, a in enumerate(parts):
+            cost += max(min(64, width(a[1])), width(a[2])) * (1 if two(a[1]) else 4) * PEC
+            if cost >= K["CUT"] or i == k - 1:
+                op("t", fns[lo:i + 1], [x for a in parts[lo:i + 1] for x in a[1:]], [out], cost, lat=0.06, grp=grp, line=bufof(out))
+                lo, cost = i + 1, 0.0
 
-    def load(dst, src, nbytes, lo=0, hi=None):
-        op("s", lambda e: e.dma_start(ap(dst), T[src][:, lo:hi] if hi else T[src][:]), [], [dst], 0.06, kind="load", bytes=nbytes)
+    def load(dst, src, nbytes):
+        op("s", lambda e: e.dma_start(ap(dst), T[src][:]), [], [dst], 0.05, kind="load", bytes=nbytes)
 
-    def fill(x, val):
-        op("v", lambda e: e.memset(ap(x), val), [], [x], vc(width(x) * 0.5))
+    def fill(x, val, p0=0, p1=128):
+        buf, lo, hi, st = norm(x)
+        op("v", lambda e: e.memset(T[buf][p0:p1, lo:hi:st] if st > 1 else T[buf][p0:p1, lo:hi], val), [], [x], vc(width(x) * (0.5 if two(x) else 1)))
 
     def sel(out, a, pat, base, cm, cmp=A.is_ge, other=0.0):
         op("c", lambda e: e.affine_select(ap(out), ap(a), pat, cmp, other, base, cm), [a], [out], 0.17 + 2 * width(out) * CYC)
@@ -274,236 +447,248 @@ def make(core, nxt, prv, T, topo):
     def iota(out, pat, base, cm):
         op("c", lambda e: e.iota(ap(out), pat, base, cm, allow_small_or_imprecise_dtypes=True), [], [out], 0.13 + 2 * width(out) * CYC)
 
-    load("JM", "jm", 4096)
-    load("JT", "jt", 128 * 768 * 4)
-    load(("D", 3840, 4096), "sd", 64 << 10, 3840, 4096)
-    load("RT", "rt", 768)
-    load("LM", "lm", 128 * 768 * 2)
-    load(("X", 0, 4096), "xw", 1 << 20)
-    load("PK", "pk", 128 * 384 * 4)
-    load(("D", 0, 3840), "sd", 960 << 10, 0, 3840)
+    def col(x, lo, w=128, st=1):
+        x = (x,) if isinstance(x, str) else x
+        base = x[1] if len(x) > 1 else 0
+        return (x[0], base + lo, base + lo + (w - 1) * st + 1, st)
+
+    srcs = {"JM": ("JM", "jm", 4096), "JT": ("JT", "jt", 128 * 768 * 4), "X": (("X", 0, 4096), "xw", 1 << 20), "LM": ("LM", "lm", 128 * 768 * 2),
+            "RT": ("RT", "rt", 768), "D": ("D", "sd", 1 << 20), "PK": ("PK", "pk", 128 * 384 * 4)}
+    for x in K["LOADS"]:
+        load(*srcs[x])
 
     fill("ONE", 1.0)
-    fill("BIG", 8192.0)
-    sel("EYE", ("ONE", 0, 128), [[-1, 128]], 0, 1, A.is_equal)
+    fill("ZER", 0.0)
+    sel("EYE", "ONE", [[-1, 128]], 0, 1, A.is_equal)
     sel("G8A", ("ONE", 0, 8), [[-16, 8]], 0, 1)
     sel("G8", "G8A", [[16, 8]], 15, -1)
-    sel("BOA", ("ONE", 0, 128), [[-16, 8], [0, 16]], 0, 1)
-    sel("BO", "BOA", [[16, 8], [0, 16]], 15, -1)
-    iota("KC", [[0, 16], [-1, 16]], 15, 0)
-    iota("MM", [[128, 8]], 4096, 1)
-    sel("TRI", "BIG", [[0, 4], [-1, 128]], 0, 1)
-    iota("WI", [[1, 256]], 3840, 0)
-    fill("RST", 1.0)
-    fill(("RST", 0, 256, 32), 0.0)
+    iota("KC", [[0, 8], [-1, 16]], 15, 0)
+    iota("KG", [[-4, 8], [0, 16]], 28, 0)
+    sel("BOA", "ONE", [[-16, 8], [0, 16]], 0, 1)
+    sel(col("BO", 0), "BOA", [[16, 8], [0, 16]], 15, -1)
+    cp("v", col("BO", 128), col("BO", 0))
+    cp("v", col("BO", 256, 256), col("BO", 0, 256))
+    iota("MM", [[16, 8]], 2048, 1)
+    for b in range(2):
+        sel(col("TRI", 512 * b, 512), "ZER", [[16, 4], [0, 8], [1, 16]], 64 * b, -1, A.is_gt, 0.5)
+    fill("MONE", -1.0)
+    fill("BIG", 8192.0)
+    act("RST", "KC", AF.Sigmoid, scale=-1024.0, bias=14.5 * 1024)
+    fill(("PM", 128, 144), 0.0)
     fill("CS", 0.0)
     cp("v", ("CS", 15, 143, 16), "G8")
-    fill("DI", 0.0)
-    fill("ZER", 0.0)
-    for h in range(4):
-        sel(("EX", 512 * h, 512 * h + 512), "ZER", [[-1, 32], [0, 16]], -32 * h, 1, A.not_equal, 1.0)
-    ts(("GD", 0, 16, 2), "G8", 16.0, A.mult)
-    ts(("GD", 1, 16, 2), "G8", 16.0, A.mult)
-    for k in range(16):
-        cp("a", ("DI", k * 128 + k, k * 128 + 128, 16), ("EYE", k, 128, 16))
+    for i, n in enumerate(EYES):
+        if i % 2:
+            ts(n, "EYE", EYES[n], A.mult)
+        else:
+            act(n, "EYE", AF.Copy, scale=EYES[n])
+    act("EYE32", "EYE", AF.Copy)
+    act("NEYE32", "EYE", AF.Copy, scale=-1.0)
+    ts("GD", "G8", 16.0, A.mult)
     for h in range(2):
-        x = ("GMA", 512 * h, 512 * h + 512)
-        sel(x, "ONE", [[-16, 4], [0, 128]], -64 * h, 1)
-        sel(("GM", 512 * h, 512 * h + 512), x, [[16, 4], [0, 128]], 64 * h + 15, -1)
-    act("NGM", "GM", AF.Copy, scale=-1.0)
-    act("EYE4", "EYE", AF.Copy, scale=4.0)
-    act("NEYE", "EYE", AF.Copy, scale=-1.0)
-    act("NEYE8", "EYE", AF.Copy, scale=-8.0)
+        x = col("NGM", 512 * h, 512)
+        sel(x, "ZER", [[16, 4], [0, 128]], 64 * h - 1, -1, A.is_ge, -1.0)
+        sel(x, x, [[16, 4], [0, 128]], 64 * h + 15, -1)
+    for c, big, small in (("CQ", 2.0 ** 18, (96.0, 160.0, 224.0)), ("CP", -196608.0, (-64.0, -128.0, -192.0))):
+        fill(c, big, 0, 64)
+        for i in range(3):
+            fill(col(c, 128 * i), small[i], 64, 128)
+    cp("v", col("CU", 0), col("CQ", 128))
+    fill(col("CU", 128), -2.0 ** 17)
+    fill(col("CU", 256), -32.0)
+    cp("v", "RTF", "RT")
+    ts("RT8", "RT", -1.0, A.mult, -8.0, A.add)
 
     def CS(k):
         return ("CS", 15 - k, 143 - k)
 
-    def DI(k):
-        return ("DI", 128 * k, 128 * k + 128)
+    UP12, UP14 = 1024.5 + 2.0 ** -13, 1024.625
 
     cp("v", "JL0", "JM")
-    ts("IC", "JT", 4095, A.bitwise_and)
-    cp("v", "TL", "IC")
-    ts("IB", "JT", 12, A.logical_shift_right)
-    cp("v", "NX", "IB")
-    we = ("D", 3840, 4096)
-    tt("WS", we, "WI", A.add)
-    ts("WF", "WS", 4096.0, A.is_ge, -256.0, A.mult)
-    tt(we, we, "WF", A.add)
-    cp("v", "RTF", "RT")
-    ts("RT8", "RT", -1.0, A.mult, -8.0, A.add)
-    ts("M0", "PK", 4095, A.bitwise_and)
-    ts("M3", "M0", -3.0, A.mult)
+    cp("v", "JF", "JT")
+    ts("TL", "JT", 4095, A.bitwise_and)
+    cp("v", "PKF", "PK")
+    act("F0", "PKF", AF.Copy, scale=1.0 / 4096, bias=UP12)
     for i in range(3):
-        ts(("PG", 128 * i, 128 * i + 128), ("PK", 128 * i, 128 * i + 128), 4.0, A.mult, 4096.0 * (2 - i), A.add)
-    tt("Q0", "PG", "M3", A.add)
+        o = col("p7", 128 * i)
+        mm(o, [(o, col("F0", 128 * i), "E12K"), (o, "ONE", col("CP", 128 * i)), (o, col("PKF", 128 * i), "EYE32")])
+    cp("a", "Q0", ("p7", 0, 384))
 
     for t in range(NT):
         def n_(x, t=t):
             return "%s%d" % (x, t)
         last = t == NT - 1
-        JL, aL, nL, XA, OV, DG, N2 = (n_(x) for x in ("JL", "aL", "nL", "XA", "OV", "DG", "N2"))
-        Q2 = ("Q0", 256, 384) if t == 0 else "LAND%d" % (t - 1)
-        Q0, Q1, Q01 = (n_("Q"), 0, 128), (n_("Q"), 128, 256), (n_("Q"), 0, 256)
-        tA, tB, tC, tD = (("p7", 128 * i, 128 * i + 128) for i in range(4))
-        tCD = ("p7", 256, 512)
-        OHA = ("p4", 256, 384)
-        gather("v", aL, "TL", 768, JL)
+        JL, aL, nL, XA, OV, DG, N2, aH, nF, uc, t2, Q, Fh, EQ, OH = (n_(x) for x in ("JL", "aL", "nL", "XA", "OV", "DG", "N2", "aH", "nF", "uc", "t2", "Q", "Fh",
+                                                                                     "EQ", "OH"))
+        Qn = "Q%d" % (t + 1)
+        Q0, Q1, Q2, Q01 = col(Q, 0), col(Q, 128), col(Q, 256), col(Q, 0, 256)
+        e0, e1, e2 = (col(n_("e"), 128 * i) for i in range(3))
+        s0, s01 = col(n_("sg"), 0), col(n_("sg"), 128)
+        MW = n_("mw")
+        QD, WL = col("p0", 0, 256), col("p1", 256, 256)
+        MNp, REC, MWp = col("p1", 0), col("p1", 128), col("p4", 256)
+        AT = col("p2", 384)
+        DN, CNT, VT = col("p0", 128), col("p3", 0), col("p3", 128)
+        OHp = col("p4", 384)
+        DL, JLp, BOp = col("p5", 0), col("p5", 128, 8), col("p4", 128)
+        EV, UX, HI, TD, SL, OFp = col("p6", 0, 384), col("p6", 0), col("p6", 128), col("p6", 256), col(*K["SL"]), col("p5", 384, 8)
+        SI, VLp, UN = col("p7" if t == 0 else "p3", 256), col("p5", 288, 8), col("p7", 0)
+        JLp = col("p0", 256, 8)
+        tA, tQ = col("p5", 144), col("p7", 256, 256)
+        if t == 0:
+            op("v", lambda e: e.tensor_scalar(ap("aI0"), T.JT[:, 0:768].indirect(ap("JL0")), 4095, None, A.bitwise_and), ["JT", "JL0"], ["aI0"], 0.22)
+            cp("v", aL, "aI0")
+            gather("v", nF, "JT", 768, JL, mul=1.0 / 4096, add=UP12)
+        else:
+            gather("v", aL, "TL", 768, JL)
+            gather("a", nF, "JF", 768, JL, "g", mul=1.0 / 4096, add=UP12)
+        ts(nL, nF, -1025.0, A.add)
+        ts(aH, aL, -2048.0, A.add)
         gather("a", n_("Lj"), "LM", 768, JL)
-        gather("v", nL, "NX", 768, JL)
-        gather("a", n_("aF"), "TL", 768, JL)
-        gather("a", n_("nF"), "NX", 768, JL)
-        o = ("p0", 0, 128)
-        mm(o, [(o, n_("Lj"), "EYE")], [n_("Lj"), "EYE"])
-        cp("a", n_("LT"), o)
 
         def wear():
-            for q, e in enumerate(XQ[t]):
-                gather(e, (XA, 512 * q, 512 * q + 512), "X", 4096, (aL, 32 * q, 32 * q + 32), "g%d" % t)
+            for q, e in enumerate(K["XQ"][t]):
+                gather(e, col(XA, 512 * q, 512), "X", 4096, col(aL, 32 * q, 32), "g%d" % t)
 
         def dist():
-            for q, e in enumerate(DQ[t]):
-                gather(e, (DG, 512 * q, 512 * q + 512), "D", 4096, (aL, 32 * q, 32 * q + 32), "g%d" % t)
+            for q, e in enumerate(K["DQ"][t]):
+                gather(e, col(DG, 512 * q, 512), "D", 4096, col(aL, 32 * q, 32), "g%d" % t)
 
         def second():
-            for q, e in enumerate(NQ[t]):
-                gather(e, (N2, 512 * q, 512 * q + 512), "NX", 768, (nL, 32 * q, 32 * q + 32), "g%d" % t)
-        for y in ORDER[t]:
+            for q, e in enumerate(K["NQ"][t]):
+                gather(e, col(N2, 512 * q, 512), "JF", 768, col(nL, 32 * q, 32), "g%d" % t, mul=1.0 / 4096, add=UP12)
+        for y in K["ORDER"][t]:
             {"d": dist, "n": second, "x": wear}[y]()
-        for q in range(4):
-            c, b = (XA, 512 * q, 512 * q + 512), "p%d" % (q // 2)
-            o, x = (OV, 512 * q, 512 * q + 512), ("EX", 512 * q, 512 * q + 512)
-            if CQ[t][q // 2] == "v":
-                mm(b, [(b, n_("LT"), x)], [n_("LT"), x])
-                tt(o, c, b, A.is_gt)
-            else:
-                mm(b, [(b, n_("LT"), x), (b, "NEYE", c)], [n_("LT"), x, "NEYE", c])
-                act(o, b, AF.Sign, scale=-1.0, bias=-0.5)
-        k2 = ("p4", 0, 256)
-        mm(k2, [(k2, "EYE", "KC")], ["EYE", "KC"], stop=False, grp="k%d" % t)
-        mm(k2, [(("p4", k, 256, 16), (XA, k, 2048, 16), "GD") for k in range(16)], [XA, "GD"], start=False, grp="k%d" % t)
-        op("v", lambda e, x=n_("pm"): e.tensor_tensor_scan(ap(x), ap("RST"), ap(("p4", 0, 256)), 0.0, A.mult, A.max), ["RST", k2], [n_("pm")], vc(256))
-        op("v", lambda e, t=t: e.tensor_tensor(T["E3%d" % t][:, :, :], ap(("p4", 0, 256)), ap("pm%d" % t), A.is_equal), [k2, n_("pm")], ["E3%d" % t], vc(256))
-        op("a", lambda e, t=t: e.activation(ap("OH%d" % t), T["E3%d" % t][:, :, 16:32], AF.Copy), ["E3%d" % t], [n_("OH")], 0.18)
-        mm(OHA, [(OHA, n_("OH"), "EYE")], [n_("OH"), "EYE"])
         for h in range(2):
-            o = ("p5", 64 * h, 64 * h + 64)
-            mm(o, [(o, CS(k), (OV, 1024 * h + k, 1024 * h + 1024, 16)) for k in range(16)], ["CS", (OV, 1024 * h, 1024 * h + 1024)])
-        for h in range(2):
-            ts((n_("cS"), 64 * h, 64 * h + 64), ("p5", 64 * h, 64 * h + 64), 8.5 if CQ[t][h] == "v" else 1.0, A.is_ge)
-
-        def pick_n():
-            for h in range(2):
-                o = ("p2", 64 * h, 64 * h + 64)
-                mm(o, [(o, DI(k), (N2, 1024 * h + k, 1024 * h + 1024, 16)) for k in range(16)] + [(o, "NEYE", (n_("nF"), 64 * h, 64 * h + 64))],
-                   ["DI", (N2, 1024 * h, 1024 * h + 1024), "NEYE", n_("nF")])
-
-        def pick_d():
-            for h in range(2):
-                o = ("p6", 64 * h, 64 * h + 64)
-                mm(o, [(o, DI(k), (DG, 1024 * h + k, 1024 * h + 1024, 16)) for k in range(16)], ["DI", (DG, 1024 * h, 1024 * h + 1024)])
-        for f in ((pick_n, pick_d) if t == 0 else (pick_d, pick_n)):
-            f()
-        act(n_("ws"), ("p6", 0, 128), AF.Sign, bias=0.5)
-        act(n_("wr"), n_("ws"), AF.Copy, scale=1920.0, bias=-1920.0)
-        tt(tC, ("p6", 0, 128), n_("wr"), A.add)
-        tt(tA, n_("cS"), ("p2", 0, 128), A.mult)
-        tt(n_("nN"), tA, n_("nF"), A.add)
-        if not last:
-            tt(n_("MN"), n_("nN"), OHA, A.mult)
-            mm(("p4", 0, 8), [(("p4", 0, 8), CS(k), (n_("MN"), k, 128, 16)) for k in range(16)], ["CS", n_("MN")])
-            cp("v", "JL%d" % (t + 1), ("p4", 0, 8))
-            scatter("NX", 768, JL, n_("nN"))
-        tt(tC, n_("cS"), tC, A.mult)
-        tt(tB, tC, n_("aF"), A.add)
-        tt(n_("U"), tC, n_("aF"), A.add)
-        act(n_("Uc"), n_("U"), AF.Identity, bias=-2048.0)
-        if not last:
-            scatter("TL", 768, JL, n_("U"))
-        if t:
-            ts((n_("M"), 256, 384), Q2, 4095, A.bitwise_and)
-        tt(tD, Q0, Q1, A.max)
-        tt(n_("EQ"), tD, Q2, A.max)
-        r0, r1 = (n_("r"), 0, 128), (n_("r"), 128, 256)
-        tt(r0, Q0, n_("EQ"), A.is_equal)
-        tt(r1, Q1, n_("EQ"), A.is_equal)
-        ts(n_("evM"), n_("EQ"), 4095, A.bitwise_and)
-        ts(n_("evS"), n_("EQ"), 0xFFCFFF, A.bitwise_and)
-        tt(tD, n_("evS"), Q2, A.subtract)
-        e0, e1, e2 = ((n_("e"), 128 * i, 128 * i + 128) for i in range(3))
+            b = "p%d" % h
+            lim = [(col(b, k, 64, 8), "EYE", col(n_("Lj"), 64 * h, 64)) for k in range(8)]
+            fresh = False
+            for j in range(2):
+                c, o = col(XA, 1024 * h + j, 512, 2), [lambda h=h, j=j, t=t: T["OV%d" % t][:, 1024 * h + j:1024 * h + 1024:2], ("OV%d.%d" % (t, j), h, h + 1), 512]
+                if K["CQ"][t][2 * h + j] == "v":
+                    if not fresh:
+                        mm(b, lim, each=True)
+                        fresh = True
+                    tt(o, c, b, A.is_gt)
+                else:
+                    b2 = b if K["CQ"][t][2 * h:2 * h + 2] == "aa" and j == 0 else "p7"
+                    mm(b2, [(col(b2, k, 64, 8),) + lim[k][1:] for k in range(8)], stop=False, grp="l%d%d%d" % (t, h, j))
+                    mm(b2, [(b2, "NEYE", c)], start=False, grp="l%d%d%d" % (t, h, j))
+                    act(o, b2, AF.Sigmoid, scale=-1024.0, bias=-512.0)
+        act(Fh, Q, AF.Copy, scale=1.0 / 16384, bias=UP14)
+        for i in range(3):
+            o = col("p2", 128 * i)
+            mm(o, [(o, "ONE", col("CQ", 128 * i)), (o, "N16K", col(Fh, 128 * i)), (o, "EYE32", col(Q, 128 * i)), (o, aH, "NEYE")])
+        mm(AT, [(AT, aH, "EYE")])
+        tt(tA, Q0, Q1, A.max)
+        tt(EQ, tA, Q2, A.max)
+        act(n_("Fe"), EQ, AF.Copy, scale=1.0 / 16384, bias=UP14)
+        mm(SL, [(SL, "ONE", col("CQ", 128)), (SL, "N16K", n_("Fe")), (SL, "EYE32", EQ)])
+        act(s0, SL, AF.Sign, bias=-2047.5)
+        act(s01, SL, AF.Sign, bias=2048.5)
+        mm(EV, [(EV, "ONE", "CU"), (UX, "N16K", n_("Fe")), (UX, "EYE32", EQ), (TD, "EYE32", EQ), (UX, "N2K", s0), (TD, "N2K", s0),
+                (UX, "N2K", s01), (TD, "N2K", s01)], stop=False, grp="u%d" % t)
+        mm(SI, [(SI, aH, "EYE")], stop=False, grp="s%d" % t)
+        mm(SI, [(col(SI, k, 8, 16), col(DG, k, 128, 16), col("EYE", k, 8, 16)) for k in range(16)], start=False, grp="s%d" % t)
+        act(n_("ws"), SI, AF.Sign, bias=-2047.5)
+        mm(DL, [(DL, "N2K", "ONE")] + [(col(DL, k, 8, 16), col(DG, k, 128, 16), col("EYE", k, 8, 16)) for k in range(16)], stop=False, grp="d%d" % t)
+        mm(DL, [(DL, "N2K", n_("ws"))], start=False, grp="d%d" % t)
+        mm(DN, [(DN, nF, "NEYE")], stop=False, grp="n%d" % t)
+        mm(DN, [(col(DN, k, 8, 16), col(N2, k, 128, 16), col("EYE", k, 8, 16)) for k in range(16)], start=False, grp="n%d" % t)
+        KEY = col("p4", 0)
+        mm(KEY, [(KEY, "EYE", "KC"), (KEY, "E16K", "KG")], stop=False, grp="k%d" % t)
+        mm(KEY, [(col(KEY, k, 8, 16), col(XA, k, 128, 16), "GD") for k in range(16)], start=False, grp="k%d" % t)
+        for o, x in ((col("PM", 0), KEY), ("PN", col("PM", 15))):
+            op("v", lambda e, o=o, x=x: e.tensor_tensor_scan(ap(o), ap("RST"), ap(x), 0.0, A.mult, A.max), ["RST", x], [o], vc(128))
+        tt(OH, KEY, "PN", A.is_equal)
+        mm(OHp, [(OHp, OH, "EYE")])
+        cp("a", n_("OHN"), OHp)
+        for j in range(2):
+            mm(CNT, [(col(CNT, k, 8, 16), [lambda k=k, t=t: T["OV%d" % t][:, k:2048:16], ("OV%d.%d" % (t, j), 0, 2), 128], "G8") for k in range(j, 16, 2)],
+               each=True, grp="c%d" % t)
+        ts(n_("cS"), CNT, 8.5, A.is_ge)
+        tt(t2, n_("cS"), DN, A.mult)
+        tt(n_("t1"), n_("cS"), DL, A.mult)
         for i, x in enumerate((e0, e1, e2)):
-            tt(x, (n_("M"), 128 * i, 128 * i + 128), tB, A.is_equal)
-        o = ("p5", 128, 256)
-        mm(o, [(o, "EYE", e0), (o, "EYE", e1), (o, "EYE", e2)], ["EYE", n_("e")])
-        act(n_("ms"), o, AF.Relu, scale=-1.0, bias=1.0)
-        tt(n_("ux"), n_("evM"), tB, A.subtract)
-        tt(tC, n_("ux"), OHA, A.mult)
-        tt(n_("y1"), n_("Uc"), OHA, A.mult)
-        tt(tC, n_("ms"), tC, A.mult)
-        tt(n_("MV"), tC, n_("y1"), A.add)
-        tt(n_("MW"), n_("ms"), OHA, A.mult)
+            tt(x, col("p2", 128 * i), n_("t1"), A.is_equal)
+        tt(uc, n_("t1"), AT, A.add)
+        if not last:
+            mm(MNp, [(MNp, "EYE", nF), (MNp, OH, "E1K"), (MNp, t2, "EYE")])
+            act(n_("MN"), MNp, AF.Relu, bias=-2049.0)
+            mm(JLp, [(JLp, CS(k), col(n_("MN"), k, 8, 16)) for k in range(16)])
+            cp("v", "JL%d" % (t + 1), JLp)
+            mm(REC, [(REC, "EYE", nF), (REC, t2, "EYE")])
+            act(n_("rec"), REC, AF.Copy, scale=4096.0, bias=-4096.0 * 1025)
+            scatter("JF", 768, JL, n_("rec"))
+            mm(UN, [(UN, uc, "EYE")])
+            act(n_("un"), UN, AF.Copy, bias=2048.0)
+            scatter("TL", 768, JL, n_("un"))
+        for i, x in enumerate((e0, e1, e2)):
+            mm(EV, [(HI, "E32M", x), (UX, "N16M", x), (TD, "N16M", x)], start=False, stop=i == 2, grp="u%d" % t)
+        tt(n_("tv"), uc, HI, A.min)
+        tt(n_("vc"), n_("tv"), UX, A.max)
+        mm(VT, [(VT, n_("vc"), "EYE")])
+        tt(n_("MV"), VT, n_("OHN"), A.mult)
+        mm(MWp, [(MWp, OH, "EYE")] + [(MWp, x, "NEYE") for x in (e0, e1, e2)])
+        act(MW, MWp, AF.Relu)
         for b in range(2):
             o = "p%d" % (2 + b)
-            mm(o, [(o, "EYE", "TRI")], ["EYE", "TRI"], stop=False, grp="e%d%d" % (t, b))
-            mm(o, [(o, n_("MV"), ("NGM", 512 * b, 512 * b + 512))] +
-               [((o, 128 * x, 128 * x + 128), ("GM", 128 * (4 * b + x), 128 * (4 * b + x) + 128), n_("MV")) for x in range(4)],
-               [n_("MV"), "NGM", "GM"], start=False, grp="e%d%d" % (t, b))
-        o = ("p4", 8, 16)
-        mm(o, [(o, CS(k), (n_("MV"), k, 128, 16)) for k in range(16)], ["CS", n_("MV")])
-        ts(n_("VL"), o, 2048.0, A.add)
-        act(n_("VF"), o, AF.Identity, bias=2048.0)
-        o = ("p1", 0, 128)
-        mm(o, [(o, "BO", n_("MW"))], ["BO", n_("MW")])
-        op("a", lambda e, t=t: e.activation(ap("dl%d" % t), ap(("p1", 0, 128)), AF.Identity, bias=ap(("RTF", t, t + 1)), scale=ap(("RT8", t, t + 1))),
-           [o, "RTF", "RT8"], [n_("dl")], 0.18)
-        for x in range(8):
-            o = ("p%d" % (2 + x // 4), 128 * (x % 4), 128 * (x % 4) + 128)
-            if EB[t][x // 4] == "v":
-                op("v", lambda e, x=x, t=t, o=o: e.tensor_scalar(T["EE%d" % t][:, :, 16 * x:16 * x + 16], ap(o), 0.0, None, A.is_equal), [o], [], 0.16)
+            pen = [] if K["EB"][t][b] == "v" else [(o, "EYE", col("TRI", 512 * b, 512))]
+            mm(o, [(o, n_("MV"), "BO")] + pen +
+               [([lambda o=o, x=x: T[o][:, :, 16 * x:16 * x + 16], (o, 0, 512), 64], col("NGM", 128 * x), col(n_("MV"), 64 * b, 64)) for x in range(8)])
+        tt(n_("g1"), Q2, HI, A.min)
+        tt(n_("GV"), n_("g1"), TD, A.max)
+        mm(VLp, [(VLp, CS(k), col(n_("MV"), k, 8, 16)) for k in range(16)])
+        ts(n_("VL"), VLp, 2048.0, A.add)
+        cp(K["VH"], n_("VH"), VLp)
+        mm(BOp, [(BOp, col("BO", 0), MW)])
+        op("a", lambda e, t=t, BOp=BOp: e.activation(ap("dl%d" % t), ap(BOp), AF.Identity, bias=ap(("RTF", t, t + 1)), scale=ap(("RT8", t, t + 1))),
+           [BOp, "RTF", "RT8"], [n_("dl")], 0.17)
+        for b in range(2):
+            EE = col(n_("EE"), 512 * b, 512)
+            if K["EB"][t][b] == "v":
+                tt(EE, "p%d" % (2 + b), col("TRI", 512 * b, 512), A.is_equal)
             else:
-                if x % 4 == 0:
-                    act(n_("ab"), "p%d" % (2 + x // 4), AF.Abs)
-                o = (n_("ab"), 128 * (x % 4), 128 * (x % 4) + 128)
-                op("a", lambda e, x=x, t=t, o=o: e.activation(T["EE%d" % t][:, :, 16 * x:16 * x + 16], ap(o), AF.Relu, scale=-1.0, bias=1.0), [o], [], 0.18)
-            ops[-1]["acc"].append(("EE%d" % t, x, x + 1, True))
+                act(n_("ab"), "p%d" % (2 + b), AF.Square)
+                act(EE, n_("ab"), AF.Relu, scale=-4.0, bias=1.0)
         op("v", lambda e, t=t: e.tensor_tensor(ap("xg%d" % t), T.X[:, 0:4096].indirect(ap("VL%d" % t)), ap("dl%d" % t), A.add),
            [("X", 0, 4096), n_("VL"), n_("dl")], [n_("xg")], 0.22)
         ts(n_("xc"), n_("xg"), 0.0, A.max, 255.0, A.min)
-        o = ("p4", 16, 24)
-        mm(o, [(("p4", 16 + c, 17 + c), [lambda c=c, t=t: T["EE%d" % t][:, c, :]], ("BIG", 0, 1)) for c in range(8)], ["EE%d" % t, "BIG"], each=True)
-        tt(n_("OFa"), o, "MM", A.min)
-        tt(n_("OFb"), n_("OFa"), n_("VF"), A.max)
-        cp("v", n_("OF"), n_("OFb"))
+        mm(OFp, [(OFp, "EYE", n_("VH"))], stop=False, grp="o%d" % t)
+        for b in K["EO"]:
+            mm(OFp, [(col(OFp, c, 1), col(n_("EE"), 128 * c), ("BIG", 0, 1)) for c in range(4 * b, 4 * b + 4)], start=False, stop=b == K["EO"][1], grp="o%d" % t)
+        tt(n_("OFa"), OFp, "MM", A.min)
+        ts(n_("OF"), n_("OFa"), 2048.0, A.add)
         scatter("X", 4096 + TRASH, n_("OF"), n_("xc"))
-        tt(tD, n_("ms"), tD, A.mult)
-        tt(n_("GV"), tD, Q2, A.add)
         out = topo.engines(core, nxt)[:8]
         rin = topo.engines(prv, core)[:8]
         rid, pid = topo.addr(nxt)[:2]
-        op("c", lambda e, t=t, rid=rid, pid=pid, m=sum(1 << x for x in out): e.remote_dma(
-            T["LAND%d" % t][:], T["GV%d" % t][:], T.sem["arr%d" % t], T.sem["loc%d" % t], pid, rid, m),
+        land = col(Qn, 256)
+        op("c", lambda e, t=t, land=land, rid=rid, pid=pid, m=sum(1 << x for x in out): e.remote_dma(
+            ap(land), T["GV%d" % t][:], T.sem["arr%d" % t], T.sem["loc%d" % t], pid, rid, m),
            [n_("GV")], [("SENT%d" % t, 0, 1)], 0.3, kind="remote", lat=2.0, sem="loc%d" % t, val=len(out))
-        op("z%d" % t, None, [("SENT%d" % t, 0, 1)], ["LAND%d" % t], 0.0, kind="arrive", lat=2.0, sem="arr%d" % t, val=len(rin))
-        act(n_("qn"), n_("nN"), AF.Copy, scale=16384.0)
-        tt(n_("q"), n_("qn"), tB, A.add)
-        act(("p3", 0, 128), n_("q"), AF.Identity, bias=8192.0)
-        act(("p3", 128, 256), n_("q"), AF.Identity, bias=4096.0)
-        o = ("p5", 256, 384)
-        mm(o, [(o, "EYE4", e0), (o, "NEYE", e1), (o, "NEYE", e2), (o, "EYE", r0)], ["EYE4", "NEYE", "EYE", n_("e"), n_("r")])
-        o = ("p5", 384, 512)
-        mm(o, [(o, "NEYE8", e0), (o, "EYE4", e1), (o, "NEYE", e2), (o, "EYE", r1)], ["EYE4", "NEYE8", "NEYE", "EYE", n_("e"), n_("r")])
-        ts(n_("w"), ("p5", 256, 512), 0.5, A.is_ge)
-        tt(tCD, ("p3", 0, 256), Q01, A.subtract)
-        tt(tCD, n_("w"), tCD, A.mult)
-        tt(("Q%d" % (t + 1), 0, 256), tCD, Q01, A.add)
-        if not last:
-            ts(("M%d" % (t + 1), 0, 256), ("Q%d" % (t + 1), 0, 256), 4095, A.bitwise_and)
+        op("z%d" % t, None, [("SENT%d" % t, 0, 1)], [land], 0.0, kind="arrive", lat=1.0, sem="arr%d" % t, val=len(rin))
+        for i in range(2):
+            o = col(QD, 128 * i)
+            mm(o, [(o, nF, "E16K"), (o, "MONE", col("CQ", 128 * i)), (o, "NEYE32", col(Q, 128 * i)), (o, "E16K", t2), (o, "EYE", uc)])
+        o = col(WL, 0)
+        mm(o, [(o, "EYE", s0), (o, "E8", e0), (o, "N2", e1), (o, "N2", e2)])
+        o = col(WL, 128)
+        mm(o, [(o, "EYE", s01), (o, "NEYE", s0), (o, "N16", e0), (o, "E8", e1), (o, "N2", e2)])
+        if K["WQ"][t] == "v":
+            ts(n_("w"), WL, 0.5, A.is_ge)
+        else:
+            act(n_("w"), WL, AF.Sigmoid, scale=1024.0, bias=-512.0)
+        tt(tQ, n_("w"), QD, A.mult)
+        tt(col(Qn, 0, 256), tQ, Q01, A.add)
 
-    for src, lo, hi in ((("Q%d" % NT, 0, 256), 0, 256), ("LAND%d" % (NT - 1), 256, 384)):
-        ts(("PF", lo, hi), src, 0xFFC000, A.bitwise_and)
-        ts(("PM", lo, hi), src, 4095, A.bitwise_and)
-        ts(("PG", lo, hi), ("PF", lo, hi), 0.25, A.mult)
-        tt(("YP", lo, hi), ("PG", lo, hi), ("PM", lo, hi), A.add)
-    op("s", lambda e: e.dma_start(T.yx[:], ap(("X", 0, 4096))), [("X", 0, 4096)], [("OUTX", 0, 1)], 0.06, kind="dma", bytes=1 << 20, lat=7.0)
-    op("s", lambda e: e.dma_start(T.yp[:], ap("YP")), ["YP"], [("OUTP", 0, 1)], 0.06, kind="dma", bytes=128 * 384 * 4, lat=3.0)
+    Q, Fh = "Q%d" % NT, "Fh%d" % NT
+    for lo, w, b in ((0, 256, "p0"), (256, 128, "p1")):
+        act(col(Fh, lo, w), col(Q, lo, w), AF.Copy, scale=1.0 / 16384, bias=UP14)
+        for c in range(lo, lo + w, 128):
+            o = col(b, c)
+            mm(o, [(o, col(Fh, c), "N12K"), (o, "MONE", col("CP", c)), (o, col(Q, c), "EYE32")])
+        cp("a", col("YP", lo, w), col(b, lo, w))
+    op("s", lambda e: e.dma_start(T.yx[:], ap(("X", 0, 4096))), [("X", 0, 4096)], [("OUTX", 0, 1)], 0.06, kind="dma", bytes=1 << 20, tail=7.0)
+    op("s", lambda e: e.dma_start(T.yp[:], ap("YP")), ["YP"], [("OUTP", 0, 1)], 0.06, kind="dma", bytes=128 * 384 * 4, tail=3.0)
     return ops

from concourse.mybir import AluOpType as A, ActivationFunctionType as AF

NT = 3
TRASH = 256
PB = ["p%d" % i for i in range(8)]
SCRATCH = {p: ("psum", [128, 4, 128] if p in ("p2", "p3") else [128, 512], "float32") for p in PB}
WHERE = {}


def _own(name, cols, dtype):
    SCRATCH[name] = ("sbuf", [128, cols], dtype)
    WHERE[name] = (name, 0, cols)


def _arena(buf, dtype, pieces):
    c = 0
    for name, w in pieces:
        WHERE[name] = (buf, c, w)
        c += (w + 15) // 16 * 16
    SCRATCH[buf] = ("sbuf", [128, c], dtype)


EYES = {"NEYE": -1.0, "N2": -2.0, "E8": 8.0, "N16": -16.0, "E1K": 1024.0, "N2K": -2048.0, "E4K": 4096.0, "E12K": 12288.0, "N12K": -12288.0,
        "E16K": 16384.0, "N16K": -16384.0, "N16M": -2.0 ** 24, "E32M": 2.0 ** 25}
for _n, _w, _d in (("X", 4096 + TRASH, "bfloat16"), ("D", 4096, "bfloat16"), ("LM", 768, "bfloat16"), ("RT", 3, "bfloat16"), ("JT", 768, "int32"),
                   ("PK", 384, "int32"), ("JM", 8, "int32"), ("JF", 768, "float32"), ("TL", 768, "int32"), ("PKF", 384, "float32"), ("F0", 384, "float16"), ("YP", 384, "float32")):
    _own(_n, _w, _d)
_arena("cb", "bfloat16", [("ONE", 128), ("MONE", 128), ("ZER", 512), ("BIG", 16), ("TRI", 1024), ("EYE", 128), ("G8A", 8), ("G8", 8), ("BOA", 128), ("BO", 512),
                          ("NGM", 1024), ("CS", 144), ("KC", 128), ("KG", 128), ("GD", 8), ("CQ", 384), ("CP", 384), ("CU", 384), ("RST", 128)] + [(n, 128) for n in EYES])
_arena("cf", "float32", [("EYE32", 128), ("NEYE32", 128), ("PM", 144), ("PN", 128), ("MM", 8), ("RTF", 3), ("RT8", 3)])
for _t in range(NT):
    for _n, _w, _d in (("XA", 2048, "bfloat16"), ("OV", 2048, "bfloat16"), ("DG", 2048, "bfloat16"), ("N2", 2048, "float16"), ("GV", 128, "float32")):
        _own("%s%d" % (_n, _t), _w, _d)
    _own("EE%d" % _t, 1024, "bfloat16")
    _arena("u%d" % _t, "uint16", [("%s%d" % (n, _t), w) for n, w in (("JL", 8), ("aL", 128), ("nL", 128), ("VL", 8), ("OF", 8))])
    _arena("f%d" % _t, "float32", [("%s%d" % (n, _t), w) for n, w in (("cS", 128), ("t1", 128), ("EQ", 128), ("tv", 128), ("g1", 128), ("ab", 512), ("rec", 128), ("un", 128),
                                                                       ("OFa", 8))])
    _arena("i%d" % _t, "int32", [("%s%d" % (n, _t), w) for n, w in (("rI", 128), ("aI", 128))])
    _arena("b%d" % _t, "bfloat16", [("%s%d" % (n, _t), w) for n, w in (("Lj", 128), ("OH", 128), ("OHN", 128), ("e", 384), ("sg", 256), ("mw", 128), ("w", 256), ("xc", 128),
                                                                       ("ws", 128), ("dl", 128))])
    _arena("h%d" % _t, "float16", [("%s%d" % (n, _t), w) for n, w in (("MN", 128), ("MV", 128), ("nF", 128), ("aH", 128), ("uc", 128), ("t2", 128), ("Fe", 128),
                                                                      ("xg", 128), ("vc", 128), ("VH", 8))])
for _t in range(NT + 1):
    _own("Q%d" % _t, 384, "float32")
    _own("Fh%d" % _t, 384, "float16")
SEMAPHORES = ["v", "a", "t", "c"] + ["d%d" % i for i in range(24)] + ["arr%d" % t for t in range(NT)] + ["loc%d" % t for t in range(NT)]

K = {"XQ": ("avav", "vvaa", "vvaa"), "DQ": ("avav", "aaaa", "aaaa"), "NQ": ("vava", "aaaa", "aaaa"), "CQ": ("vvvv", "vvva", "vvva"), "EB": ("vv", "vv", "vv"),
     "CUT": 0.2, "WQ": "aaa", "VH": "a", "SL": ("p6", 384), "EO": (0, 1), "ORDER": ("nxd", "ndx", "dxn"), "SEED": 1, "TOL": 0.08, "MOVES": 250000, "HEAT": 0.4, "PULL": 0.003,
     "WEIGHT": (1.0, 0.5), "LOADS": ("JM", "JT", "X", "LM", "PK", "RT", "D")}
CYC = 0.83e-3
PEC = 0.42e-3
GUESS = ((1.0, 1.56, 3.8, 0.10, 0.05, 250e3), (1.3, 1.3, 5.0, 0.2, 0.1, 300e3), (1.0, 1.2, 2.5, 0.06, 0.03, 350e3))
PLAN = {}


def plan(ops, pred, soft):
    n = len(ops)
    succ = [[] for _ in range(n)]
    left0 = [len(p) for p in pred]
    for i in range(n):
        for j in pred[i]:
            succ[j].append(i)
        if soft[i] is not None and soft[i] not in pred[i]:
            succ[soft[i]].append(i)
            left0[i] += 1
    isdma = [o["kind"] in ("load", "dma") for o in ops]
    lat = [o["lat"] for o in ops]
    cost = [[(o["fix"] + o["cyc"] * {"g": m[1], "s": m[2]}.get(o["per"], 1.0)) * (1.0 if o["kind"] != "op" else m[0]) for o in ops] for m in GUESS]
    flex = [bool(o.get("alt")) for o in ops]

    def finish(i, st, m, link):
        if isdma[i]:
            link[0] = max(link[0], st + 1.5) + ops[i]["bytes"] / GUESS[m][5]
            return link[0] + 0.5
        return st + cost[m][i] + lat[i]

    def schedule(prio, qs):
        w, ws = GUESS[0][3:5]
        left = list(left0)
        done = [0.0] * n
        at = [0.0] * n
        free = {q: 0.0 for q in qs}
        ready = {q: [] for q in qs}
        for i in range(n):
            if not left[i]:
                ready[qs[i]].append(i)
        link = [0.0]
        order = []
        tol = K["TOL"]
        while len(order) < n:
            est, q = min((max(free[q], min([at[i] for i in r])), q) for q, r in ready.items() if r)
            lim = est + tol
            pick = max([i for i in ready[q] if at[i] <= lim], key=lambda i: prio[i])
            ready[q].remove(pick)
            st = max(free[q], at[pick])
            free[q] = st + cost[0][pick]
            done[pick] = finish(pick, st, 0, link)
            order.append(pick)
            for s in succ[pick]:
                left[s] -= 1
                if not left[s]:
                    at[s] = max([done[j] + (ws if qs[j] == qs[s] else w) for j in pred[s]] + [0.0])
                    ready[qs[s]].append(s)
        return order, max(done)

    names = sorted({o["q"] for o in ops})
    outs = [k for k in range(n) if ops[k]["kind"] == "dma"]

    def replay(order, qs, m, a=0, prev=None):
        w, ws, rate = GUESS[m][3:6]
        c = cost[m]
        free = dict.fromkeys(names, 0.0)
        last = dict.fromkeys(names, -1)
        link = 0.0
        if a:
            done, why = list(prev[1]), list(prev[2])
            left = 4
            for i in reversed(order[:a]):
                q = qs[i]
                if last[q] < 0:
                    last[q] = i
                    free[q] = done[i] - lat[i]
                    if isdma[i]:
                        link = done[i] - 0.5
                        free[q] = 1.0
                    if q in "vatc":
                        left -= 1
                        if not left and link:
                            break
        else:
            done = [0.0] * n
            why = [-1] * n
        for i in order[a:]:
            q = qs[i]
            st = free[q]
            y = last[q]
            for j in pred[i]:
                d = done[j] + (ws if qs[j] == q else w)
                if d > st:
                    st = d
                    y = j
            why[i] = y
            last[q] = i
            free[q] = e = st + c[i]
            if isdma[i]:
                link = max(link, st + 1.5) + ops[i]["bytes"] / rate
                done[i] = link + 0.5
            else:
                done[i] = e + lat[i]
        return max([done[k] for k in outs]) + K["PULL"] * sum(done), done, why

    prio = [0.0] * n
    after = {}
    for i in range(n - 1, -1, -1):
        prio[i] = cost[0][i] + lat[i] + ops[i].get("tail", 0.0) + max([prio[s] + GUESS[0][3] for s in succ[i]] + [0.0])
        if ops[i].get("alt") and ops[i]["cyc"] > 0.3:
            prio[i] = max(prio[i], cost[0][i] + after.get(ops[i]["q"], 0.0))
            after[ops[i]["q"]] = prio[i]
    for i in range(n):
        if ops[i]["kind"] == "load":
            prio[i] = 1e6 - 1e3 * i
    qs = [o["q"] for o in ops]
    order = schedule(prio, qs)[0]
    h = [K["SEED"]]

    def rnd():
        h[0] = (h[0] * 1103515245 + 12345) % 2147483648
        return h[0] / 2147483648.0
    allp = [pred[i] + ([soft[i]] if soft[i] is not None and soft[i] not in pred[i] else []) for i in range(n)]
    fixed = [o["kind"] in ("load", "arrive") for o in ops]
    other = {"a": "v", "v": "a"}
    W = K["WEIGHT"]
    M = range(len(W))
    cur = [replay(order, qs, m) for m in M]
    cv = sum(W[m] * cur[m][0] for m in M)
    best = (cv, order, qs)
    stale = True
    for it in range(K["MOVES"]):
        if stale:
            path = []
            for m in M:
                for i in outs:
                    while i >= 0:
                        path.append(i)
                        i = cur[m][2][i]
            pos = [0] * n
            for p, i in enumerate(order):
                pos[i] = p
            stale = False
        j = path[int(rnd() * len(path))] if rnd() < 0.6 else int(rnd() * n)
        if fixed[j]:
            continue
        q2, o2, a, b, x = qs, order, pos[j], pos[j], rnd()
        if flex[j] and x < 0.4:
            q2 = list(qs)
            q2[j] = other[qs[j]]
            near = [k for k in order[max(0, b - 40):b + 40] if flex[k] and qs[k] == q2[j]] if x < 0.2 else []
            if near:
                k = near[int(rnd() * len(near))]
                q2[k] = qs[j]
                a = min(a, pos[k])
        elif x > 0.85:
            lo = max([pos[k] for k in allp[j]] + [-1]) + 1
            p = lo + int(rnd() * (min([pos[k] for k in succ[j]] + [n]) - lo))
            if p == b:
                continue
            o2 = order[:p] + [j] + order[p:b] + order[b + 1:] if p < b else order[:b] + order[b + 1:p + 1] + [j] + order[p + 1:]
            a = min(p, b)
            if flex[j] and rnd() < 0.5:
                q2 = list(qs)
                q2[j] = other[qs[j]]
        else:
            same = [k for k in order[max(0, b - 60):b] if qs[k] == qs[j]]
            if not same:
                continue
            i = same[-1 - int(min(len(same), 6) * rnd() ** 2)]
            if fixed[i]:
                continue
            a = pos[i]
            seg = order[a:b + 1]
            if rnd() < 0.5:
                up = {j}
                for k in reversed(seg):
                    if k in up:
                        up.update(allp[k])
                if i in up:
                    continue
            else:
                dn = {i}
                for k in seg:
                    if k in dn:
                        dn.update(succ[k])
                if j in dn:
                    continue
                up = {k for k in seg if k not in dn}
            o2 = order[:a] + [k for k in seg if k in up] + [k for k in seg if k not in up] + order[b + 1:]
        if a < 20:
            a = 0
        lim = cv + K["HEAT"] * (1.0 - it / K["MOVES"]) * rnd() ** 2
        new = [replay(o2, q2, 0, a, cur[0])]
        if W[0] * (new[0][0] - cur[0][0]) > lim - cv + 0.3:
            continue
        new += [replay(o2, q2, m, a, cur[m]) for m in M[1:]]
        v = sum(W[m] * new[m][0] for m in M)
        if v <= lim:
            cur, cv, order, qs = new, v, o2, q2
            stale = True
            if v < best[0]:
                best = (v, order, qs)
    return best[1], best[2], [max(replay(best[1], best[2], m)[1]) for m in range(len(GUESS))]


def build(ops, g, T):
    n = len(ops)
    acc = {}
    chain = {}
    soft = [None] * n
    pred = [[] for _ in range(n)]
    for i, o in enumerate(ops):
        ps = set()
        for buf, lo, hi, wr in o["acc"]:
            psum = buf in PB
            for j, lo2, hi2, wr2 in acc.setdefault(buf, []):
                if (lo < hi2 and lo2 < hi and (wr or wr2)) or (psum and ops[j]["q"] != o["q"]):
                    if not (o.get("grp") and o["grp"] == ops[j].get("grp")):
                        ps.add(j)
        for buf, lo, hi, wr in o["acc"]:
            acc[buf].append((i, lo, hi, wr))
        ps.discard(i)
        pred[i] = sorted(ps)
        o["pred"] = pred[i]
        k = o.get("line")
        if k:
            soft[i] = chain.get(k)
            chain[k] = i
    if "order" not in PLAN:
        lean = []
        above = []
        for i in range(n):
            up = set()
            for j in pred[i]:
                up |= above[j]
            lean.append([j for j in pred[i] if j not in up])
            above.append(up | set(pred[i]))
        PLAN["order"], PLAN["queue"], PLAN["time"] = plan(ops, lean, soft)
    order = PLAN["order"]
    for o, q in zip(ops, PLAN["queue"]):
        if q != o["q"]:
            o["q"], o["fns"] = q, o["alt"]
    eng = {"v": g.vector, "a": g.scalar, "t": g.tensor, "c": g, "s": g.sync}
    known = {q: {} for q in eng}
    count = {q: 0 for q in eng}
    comp = [None] * n
    clock = [None] * n
    total = {}
    nd = 0
    for i in order:
        o = ops[i]
        q = o["q"]
        if o["kind"] == "arrive":
            comp[i] = (o["sem"], o["val"])
            clock[i] = {}
            total[o["sem"]] = o["val"]
            continue
        kn = known[q]
        need = {}
        for j in pred[i]:
            s, v = comp[j]
            if kn.get(s, 0) < v and need.get(s, (0, 0))[0] < v:
                need[s] = (v, j)
        for s in sorted(need, key=lambda s: -need[s][1]):
            v, j = need[s]
            if kn.get(s, 0) >= v:
                continue
            eng[q].wait_ge(T.sem[s], v)
            kn[s] = v
            for s2, v2 in clock[j].items():
                if kn.get(s2, 0) < v2:
                    kn[s2] = v2
        clock[i] = dict(kn)
        if o["kind"] in ("load", "dma"):
            s = "d%d" % nd
            nd += 1
            o["fns"][0](eng[q]).then_inc(T.sem[s], 16)
            comp[i] = (s, 16)
        elif o["kind"] == "remote":
            o["fns"][0](g)
            comp[i] = (o["sem"], o["val"])
        else:
            for f in o["fns"]:
                f(eng[q]).then_inc(T.sem[q], 1)
            count[q] += len(o["fns"])
            comp[i] = (q, count[q])
        total[comp[i][0]] = comp[i][1]
    for s in sorted(total):
        if known["c"].get(s, 0) < total[s]:
            g.wait_ge(T.sem[s], total[s])


def rank_program(g, core, T, topo):
    rank = T.rank_of(core)
    if rank is None:
        return
    nxt = T.cores[(rank + 1) % len(T.cores)]
    prv = T.cores[(rank - 1) % len(T.cores)]
    build(make(core, nxt, prv, T, topo), g, T)


def make(core, nxt, prv, T, topo):
    ops = []

    def norm(x):
        x = (x,) if isinstance(x, str) else x
        buf, c0, w = WHERE.get(x[0], (x[0], 0, 512))
        lo, hi = (x[1], x[2]) if len(x) > 1 else (0, w)
        return buf, c0 + lo, c0 + hi, (x[3] if len(x) > 3 else 1)

    def ap(x):
        if isinstance(x, list):
            return x[0]()
        buf, lo, hi, st = norm(x)
        if len(SCRATCH[buf][1]) == 3:
            return T[buf][:, lo // 128:hi // 128, :] if hi - lo > 128 else T[buf][:, lo // 128, lo % 128:(hi - 1) % 128 + 1:st]
        return T[buf][:, lo:hi:st] if st > 1 else T[buf][:, lo:hi]

    def reg(x, wr):
        if isinstance(x, list):
            return x[1] + (wr,)
        return norm(x)[:3] + (wr,)

    def op(q, fns, R, W, cost, kind="op", lat=0.0, per="", **kw):
        fix, cyc = cost if isinstance(cost, tuple) else (cost, 0.0)
        o = {"q": q, "fns": fns if isinstance(fns, list) else [fns], "acc": [reg(x, False) for x in R] + [reg(x, True) for x in W], "fix": fix, "cyc": cyc, "per": per,
             "kind": kind, "lat": lat}
        o.update(kw)
        ops.append(o)

    def width(x):
        if isinstance(x, list):
            return x[2]
        _, lo, hi, st = norm(x)
        return (hi - lo + st - 1) // st

    def bufof(x):
        return x[1][0] if isinstance(x, list) else norm(x)[0]

    def isps(x):
        return bufof(x) in PB

    def two(x):
        return SCRATCH[bufof(x).split(".")[0]][2] in ("bfloat16", "float16", "uint16")

    def vc(c):
        return 0.05 + max(64, c) * CYC

    def tt(out, a, b, o):
        op("v", lambda e: e.tensor_tensor(ap(out), ap(a), ap(b), o), [a, b], [out], vc(width(a) * (1 if isps(a) or isps(b) else 2)))

    def ts(out, a, s1, o1, s2=None, o2=None):
        c1 = (lambda: s1) if isinstance(s1, (int, float)) else (lambda: ap(s1))
        f = (lambda e: e.tensor_scalar(ap(out), ap(a), c1(), None, o1)) if o2 is None else (lambda e: e.tensor_scalar(ap(out), ap(a), c1(), s2, o1, o2))
        op("v", f, [a] + ([] if isinstance(s1, (int, float)) else [s1]), [out], vc(width(a) * (0.5 if two(a) and two(out) else 1)))

    def cp(q, out, a):
        if q == "v":
            op("v", lambda e: e.tensor_copy(ap(out), ap(a)), [a], [out], vc(width(a) * (0.5 if two(a) and two(out) else 1)))
        else:
            act(out, a, AF.Copy)

    def act(out, a, f, **kw):
        op("a", lambda e: e.activation(ap(out), ap(a), f, **kw), [a], [out], 0.065 + max(64, width(a)) * CYC)

    def gather(q, out, win, w, lst, line=None, mul=None, add=None):
        n = 16 * width(lst)
        fa = lambda e: e.activation(ap(out), T[win][:, 0:w].indirect(ap(lst)), AF.Copy, scale=mul or 1.0, bias=add or 0.0)
        if mul:
            f = lambda e: e.tensor_scalar(ap(out), T[win][:, 0:w].indirect(ap(lst)), mul, add, A.mult, A.add)
        else:
            f = lambda e: e.tensor_copy(ap(out), T[win][:, 0:w].indirect(ap(lst)))
        op(q, fa if q == "a" else f, [(win, 0, w), lst], [out], (0.06, n * CYC), per="g", alt=line and [f if q == "a" else fa])

    def scatter(win, w, lst, val):
        op("v", lambda e: e.tensor_copy(T[win][:, 0:w].indirect(ap(lst)), ap(val)), [lst, val], [(win, 0, w)], (0.05, 16 * width(lst) * CYC), per="s")

    def mm(out, parts, start=True, stop=True, each=False, grp=None):
        k = len(parts)
        fns = [(lambda e, i=i, a=a: e.matmul(ap(a[0]), ap(a[1]), ap(a[2]), each or (start and i == 0), each or (stop and i == k - 1))) for i, a in enumerate(parts)]
        grp = grp or "g%d" % len(ops)
        lo, cost = 0, 0.0
        for i, a in enumerate(parts):
            cost += max(min(64, width(a[1])), width(a[2])) * (1 if two(a[1]) else 4) * PEC
            if cost >= K["CUT"] or i == k - 1:
                op("t", fns[lo:i + 1], [x for a in parts[lo:i + 1] for x in a[1:]], [out], cost, lat=0.06, grp=grp, line=bufof(out))
                lo, cost = i + 1, 0.0

    def load(dst, src, nbytes):
        op("s", lambda e: e.dma_start(ap(dst), T[src][:]), [], [dst], 0.05, kind="load", bytes=nbytes)

    def fill(x, val, p0=0, p1=128):
        buf, lo, hi, st = norm(x)
        op("v", lambda e: e.memset(T[buf][p0:p1, lo:hi:st] if st > 1 else T[buf][p0:p1, lo:hi], val), [], [x], vc(width(x) * (0.5 if two(x) else 1)))

    def sel(out, a, pat, base, cm, cmp=A.is_ge, other=0.0):
        op("c", lambda e: e.affine_select(ap(out), ap(a), pat, cmp, other, base, cm), [a], [out], 0.17 + 2 * width(out) * CYC)

    def iota(out, pat, base, cm):
        op("c", lambda e: e.iota(ap(out), pat, base, cm, allow_small_or_imprecise_dtypes=True), [], [out], 0.13 + 2 * width(out) * CYC)

    def col(x, lo, w=128, st=1):
        x = (x,) if isinstance(x, str) else x
        base = x[1] if len(x) > 1 else 0
        return (x[0], base + lo, base + lo + (w - 1) * st + 1, st)

    srcs = {"JM": ("JM", "jm", 4096), "JT": ("JT", "jt", 128 * 768 * 4), "X": (("X", 0, 4096), "xw", 1 << 20), "LM": ("LM", "lm", 128 * 768 * 2),
            "RT": ("RT", "rt", 768), "D": ("D", "sd", 1 << 20), "PK": ("PK", "pk", 128 * 384 * 4)}
    for x in K["LOADS"]:
        load(*srcs[x])

    fill("ONE", 1.0)
    fill("ZER", 0.0)
    sel("EYE", "ONE", [[-1, 128]], 0, 1, A.is_equal)
    sel("G8A", ("ONE", 0, 8), [[-16, 8]], 0, 1)
    sel("G8", "G8A", [[16, 8]], 15, -1)
    iota("KC", [[0, 8], [-1, 16]], 15, 0)
    iota("KG", [[-4, 8], [0, 16]], 28, 0)
    sel("BOA", "ONE", [[-16, 8], [0, 16]], 0, 1)
    sel(col("BO", 0), "BOA", [[16, 8], [0, 16]], 15, -1)
    cp("v", col("BO", 128), col("BO", 0))
    cp("v", col("BO", 256, 256), col("BO", 0, 256))
    iota("MM", [[16, 8]], 2048, 1)
    for b in range(2):
        sel(col("TRI", 512 * b, 512), "ZER", [[16, 4], [0, 8], [1, 16]], 64 * b, -1, A.is_gt, 0.5)
    fill("MONE", -1.0)
    fill("BIG", 8192.0)
    act("RST", "KC", AF.Sigmoid, scale=-1024.0, bias=14.5 * 1024)
    fill(("PM", 128, 144), 0.0)
    fill("CS", 0.0)
    cp("v", ("CS", 15, 143, 16), "G8")
    for i, n in enumerate(EYES):
        if i % 2:
            ts(n, "EYE", EYES[n], A.mult)
        else:
            act(n, "EYE", AF.Copy, scale=EYES[n])
    act("EYE32", "EYE", AF.Copy)
    act("NEYE32", "EYE", AF.Copy, scale=-1.0)
    ts("GD", "G8", 16.0, A.mult)
    for h in range(2):
        x = col("NGM", 512 * h, 512)
        sel(x, "ZER", [[16, 4], [0, 128]], 64 * h - 1, -1, A.is_ge, -1.0)
        sel(x, x, [[16, 4], [0, 128]], 64 * h + 15, -1)
    for c, big, small in (("CQ", 2.0 ** 18, (96.0, 160.0, 224.0)), ("CP", -196608.0, (-64.0, -128.0, -192.0))):
        fill(c, big, 0, 64)
        for i in range(3):
            fill(col(c, 128 * i), small[i], 64, 128)
    cp("v", col("CU", 0), col("CQ", 128))
    fill(col("CU", 128), -2.0 ** 17)
    fill(col("CU", 256), -32.0)
    cp("v", "RTF", "RT")
    ts("RT8", "RT", -1.0, A.mult, -8.0, A.add)

    def CS(k):
        return ("CS", 15 - k, 143 - k)

    UP12, UP14 = 1024.5 + 2.0 ** -13, 1024.625

    cp("v", "JL0", "JM")
    cp("v", "JF", "JT")
    ts("TL", "JT", 4095, A.bitwise_and)
    cp("v", "PKF", "PK")
    act("F0", "PKF", AF.Copy, scale=1.0 / 4096, bias=UP12)
    for i in range(3):
        o = col("p7", 128 * i)
        mm(o, [(o, col("F0", 128 * i), "E12K"), (o, "ONE", col("CP", 128 * i)), (o, col("PKF", 128 * i), "EYE32")])
    cp("a", "Q0", ("p7", 0, 384))

    for t in range(NT):
        def n_(x, t=t):
            return "%s%d" % (x, t)
        last = t == NT - 1
        JL, aL, nL, XA, OV, DG, N2, aH, nF, uc, t2, Q, Fh, EQ, OH = (n_(x) for x in ("JL", "aL", "nL", "XA", "OV", "DG", "N2", "aH", "nF", "uc", "t2", "Q", "Fh",
                                                                                     "EQ", "OH"))
        Qn = "Q%d" % (t + 1)
        Q0, Q1, Q2, Q01 = col(Q, 0), col(Q, 128), col(Q, 256), col(Q, 0, 256)
        e0, e1, e2 = (col(n_("e"), 128 * i) for i in range(3))
        s0, s01 = col(n_("sg"), 0), col(n_("sg"), 128)
        MW = n_("mw")
        QD, WL = col("p0", 0, 256), col("p1", 256, 256)
        MNp, REC, MWp = col("p1", 0), col("p1", 128), col("p4", 256)
        AT = col("p2", 384)
        DN, CNT, VT = col("p0", 128), col("p3", 0), col("p3", 128)
        OHp = col("p4", 384)
        DL, JLp, BOp = col("p5", 0), col("p5", 128, 8), col("p4", 128)
        EV, UX, HI, TD, SL, OFp = col("p6", 0, 384), col("p6", 0), col("p6", 128), col("p6", 256), col(*K["SL"]), col("p5", 384, 8)
        SI, VLp, UN = col("p7" if t == 0 else "p3", 256), col("p5", 288, 8), col("p7", 0)
        JLp = col("p0", 256, 8)
        tA, tQ = col("p5", 144), col("p7", 256, 256)
        if t == 0:
            op("v", lambda e: e.tensor_scalar(ap("aI0"), T.JT[:, 0:768].indirect(ap("JL0")), 4095, None, A.bitwise_and), ["JT", "JL0"], ["aI0"], 0.22)
            cp("v", aL, "aI0")
            gather("v", nF, "JT", 768, JL, mul=1.0 / 4096, add=UP12)
        else:
            gather("v", aL, "TL", 768, JL)
            gather("a", nF, "JF", 768, JL, "g", mul=1.0 / 4096, add=UP12)
        ts(nL, nF, -1025.0, A.add)
        ts(aH, aL, -2048.0, A.add)
        gather("a", n_("Lj"), "LM", 768, JL)

        def wear():
            for q, e in enumerate(K["XQ"][t]):
                gather(e, col(XA, 512 * q, 512), "X", 4096, col(aL, 32 * q, 32), "g%d" % t)

        def dist():
            for q, e in enumerate(K["DQ"][t]):
                gather(e, col(DG, 512 * q, 512), "D", 4096, col(aL, 32 * q, 32), "g%d" % t)

        def second():
            for q, e in enumerate(K["NQ"][t]):
                gather(e, col(N2, 512 * q, 512), "JF", 768, col(nL, 32 * q, 32), "g%d" % t, mul=1.0 / 4096, add=UP12)
        for y in K["ORDER"][t]:
            {"d": dist, "n": second, "x": wear}[y]()
        for h in range(2):
            b = "p%d" % h
            lim = [(col(b, k, 64, 8), "EYE", col(n_("Lj"), 64 * h, 64)) for k in range(8)]
            fresh = False
            for j in range(2):
                c, o = col(XA, 1024 * h + j, 512, 2), [lambda h=h, j=j, t=t: T["OV%d" % t][:, 1024 * h + j:1024 * h + 1024:2], ("OV%d.%d" % (t, j), h, h + 1), 512]
                if K["CQ"][t][2 * h + j] == "v":
                    if not fresh:
                        mm(b, lim, each=True)
                        fresh = True
                    tt(o, c, b, A.is_gt)
                else:
                    b2 = b if K["CQ"][t][2 * h:2 * h + 2] == "aa" and j == 0 else "p7"
                    mm(b2, [(col(b2, k, 64, 8),) + lim[k][1:] for k in range(8)], stop=False, grp="l%d%d%d" % (t, h, j))
                    mm(b2, [(b2, "NEYE", c)], start=False, grp="l%d%d%d" % (t, h, j))
                    act(o, b2, AF.Sigmoid, scale=-1024.0, bias=-512.0)
        act(Fh, Q, AF.Copy, scale=1.0 / 16384, bias=UP14)
        for i in range(3):
            o = col("p2", 128 * i)
            mm(o, [(o, "ONE", col("CQ", 128 * i)), (o, "N16K", col(Fh, 128 * i)), (o, "EYE32", col(Q, 128 * i)), (o, aH, "NEYE")])
        mm(AT, [(AT, aH, "EYE")])
        tt(tA, Q0, Q1, A.max)
        tt(EQ, tA, Q2, A.max)
        act(n_("Fe"), EQ, AF.Copy, scale=1.0 / 16384, bias=UP14)
        mm(SL, [(SL, "ONE", col("CQ", 128)), (SL, "N16K", n_("Fe")), (SL, "EYE32", EQ)])
        act(s0, SL, AF.Sign, bias=-2047.5)
        act(s01, SL, AF.Sign, bias=2048.5)
        mm(EV, [(EV, "ONE", "CU"), (UX, "N16K", n_("Fe")), (UX, "EYE32", EQ), (TD, "EYE32", EQ), (UX, "N2K", s0), (TD, "N2K", s0),
                (UX, "N2K", s01), (TD, "N2K", s01)], stop=False, grp="u%d" % t)
        mm(SI, [(SI, aH, "EYE")], stop=False, grp="s%d" % t)
        mm(SI, [(col(SI, k, 8, 16), col(DG, k, 128, 16), col("EYE", k, 8, 16)) for k in range(16)], start=False, grp="s%d" % t)
        act(n_("ws"), SI, AF.Sign, bias=-2047.5)
        mm(DL, [(DL, "N2K", "ONE")] + [(col(DL, k, 8, 16), col(DG, k, 128, 16), col("EYE", k, 8, 16)) for k in range(16)], stop=False, grp="d%d" % t)
        mm(DL, [(DL, "N2K", n_("ws"))], start=False, grp="d%d" % t)
        mm(DN, [(DN, nF, "NEYE")], stop=False, grp="n%d" % t)
        mm(DN, [(col(DN, k, 8, 16), col(N2, k, 128, 16), col("EYE", k, 8, 16)) for k in range(16)], start=False, grp="n%d" % t)
        KEY = col("p4", 0)
        mm(KEY, [(KEY, "EYE", "KC"), (KEY, "E16K", "KG")], stop=False, grp="k%d" % t)
        mm(KEY, [(col(KEY, k, 8, 16), col(XA, k, 128, 16), "GD") for k in range(16)], start=False, grp="k%d" % t)
        for o, x in ((col("PM", 0), KEY), ("PN", col("PM", 15))):
            op("v", lambda e, o=o, x=x: e.tensor_tensor_scan(ap(o), ap("RST"), ap(x), 0.0, A.mult, A.max), ["RST", x], [o], vc(128))
        tt(OH, KEY, "PN", A.is_equal)
        mm(OHp, [(OHp, OH, "EYE")])
        cp("a", n_("OHN"), OHp)
        for j in range(2):
            mm(CNT, [(col(CNT, k, 8, 16), [lambda k=k, t=t: T["OV%d" % t][:, k:2048:16], ("OV%d.%d" % (t, j), 0, 2), 128], "G8") for k in range(j, 16, 2)],
               each=True, grp="c%d" % t)
        ts(n_("cS"), CNT, 8.5, A.is_ge)
        tt(t2, n_("cS"), DN, A.mult)
        tt(n_("t1"), n_("cS"), DL, A.mult)
        for i, x in enumerate((e0, e1, e2)):
            tt(x, col("p2", 128 * i), n_("t1"), A.is_equal)
        tt(uc, n_("t1"), AT, A.add)
        if not last:
            mm(MNp, [(MNp, "EYE", nF), (MNp, OH, "E1K"), (MNp, t2, "EYE")])
            act(n_("MN"), MNp, AF.Relu, bias=-2049.0)
            mm(JLp, [(JLp, CS(k), col(n_("MN"), k, 8, 16)) for k in range(16)])
            cp("v", "JL%d" % (t + 1), JLp)
            mm(REC, [(REC, "EYE", nF), (REC, t2, "EYE")])
            act(n_("rec"), REC, AF.Copy, scale=4096.0, bias=-4096.0 * 1025)
            scatter("JF", 768, JL, n_("rec"))
            mm(UN, [(UN, uc, "EYE")])
            act(n_("un"), UN, AF.Copy, bias=2048.0)
            scatter("TL", 768, JL, n_("un"))
        for i, x in enumerate((e0, e1, e2)):
            mm(EV, [(HI, "E32M", x), (UX, "N16M", x), (TD, "N16M", x)], start=False, stop=i == 2, grp="u%d" % t)
        tt(n_("tv"), uc, HI, A.min)
        tt(n_("vc"), n_("tv"), UX, A.max)
        mm(VT, [(VT, n_("vc"), "EYE")])
        tt(n_("MV"), VT, n_("OHN"), A.mult)
        mm(MWp, [(MWp, OH, "EYE")] + [(MWp, x, "NEYE") for x in (e0, e1, e2)])
        act(MW, MWp, AF.Relu)
        for b in range(2):
            o = "p%d" % (2 + b)
            pen = [] if K["EB"][t][b] == "v" else [(o, "EYE", col("TRI", 512 * b, 512))]
            mm(o, [(o, n_("MV"), "BO")] + pen +
               [([lambda o=o, x=x: T[o][:, :, 16 * x:16 * x + 16], (o, 0, 512), 64], col("NGM", 128 * x), col(n_("MV"), 64 * b, 64)) for x in range(8)])
        tt(n_("g1"), Q2, HI, A.min)
        tt(n_("GV"), n_("g1"), TD, A.max)
        mm(VLp, [(VLp, CS(k), col(n_("MV"), k, 8, 16)) for k in range(16)])
        ts(n_("VL"), VLp, 2048.0, A.add)
        cp(K["VH"], n_("VH"), VLp)
        mm(BOp, [(BOp, col("BO", 0), MW)])
        op("a", lambda e, t=t, BOp=BOp: e.activation(ap("dl%d" % t), ap(BOp), AF.Identity, bias=ap(("RTF", t, t + 1)), scale=ap(("RT8", t, t + 1))),
           [BOp, "RTF", "RT8"], [n_("dl")], 0.17)
        for b in range(2):
            EE = col(n_("EE"), 512 * b, 512)
            if K["EB"][t][b] == "v":
                tt(EE, "p%d" % (2 + b), col("TRI", 512 * b, 512), A.is_equal)
            else:
                act(n_("ab"), "p%d" % (2 + b), AF.Square)
                act(EE, n_("ab"), AF.Relu, scale=-4.0, bias=1.0)
        op("v", lambda e, t=t: e.tensor_tensor(ap("xg%d" % t), T.X[:, 0:4096].indirect(ap("VL%d" % t)), ap("dl%d" % t), A.add),
           [("X", 0, 4096), n_("VL"), n_("dl")], [n_("xg")], 0.22)
        ts(n_("xc"), n_("xg"), 0.0, A.max, 255.0, A.min)
        mm(OFp, [(OFp, "EYE", n_("VH"))], stop=False, grp="o%d" % t)
        for b in K["EO"]:
            mm(OFp, [(col(OFp, c, 1), col(n_("EE"), 128 * c), ("BIG", 0, 1)) for c in range(4 * b, 4 * b + 4)], start=False, stop=b == K["EO"][1], grp="o%d" % t)
        tt(n_("OFa"), OFp, "MM", A.min)
        ts(n_("OF"), n_("OFa"), 2048.0, A.add)
        scatter("X", 4096 + TRASH, n_("OF"), n_("xc"))
        out = topo.engines(core, nxt)[:8]
        rin = topo.engines(prv, core)[:8]
        rid, pid = topo.addr(nxt)[:2]
        land = col(Qn, 256)
        op("c", lambda e, t=t, land=land, rid=rid, pid=pid, m=sum(1 << x for x in out): e.remote_dma(
            ap(land), T["GV%d" % t][:], T.sem["arr%d" % t], T.sem["loc%d" % t], pid, rid, m),
           [n_("GV")], [("SENT%d" % t, 0, 1)], 0.3, kind="remote", lat=2.0, sem="loc%d" % t, val=len(out))
        op("z%d" % t, None, [("SENT%d" % t, 0, 1)], [land], 0.0, kind="arrive", lat=1.0, sem="arr%d" % t, val=len(rin))
        for i in range(2):
            o = col(QD, 128 * i)
            mm(o, [(o, nF, "E16K"), (o, "MONE", col("CQ", 128 * i)), (o, "NEYE32", col(Q, 128 * i)), (o, "E16K", t2), (o, "EYE", uc)])
        o = col(WL, 0)
        mm(o, [(o, "EYE", s0), (o, "E8", e0), (o, "N2", e1), (o, "N2", e2)])
        o = col(WL, 128)
        mm(o, [(o, "EYE", s01), (o, "NEYE", s0), (o, "N16", e0), (o, "E8", e1), (o, "N2", e2)])
        if K["WQ"][t] == "v":
            ts(n_("w"), WL, 0.5, A.is_ge)
        else:
            act(n_("w"), WL, AF.Sigmoid, scale=1024.0, bias=-512.0)
        tt(tQ, n_("w"), QD, A.mult)
        tt(col(Qn, 0, 256), tQ, Q01, A.add)

    Q, Fh = "Q%d" % NT, "Fh%d" % NT
    for lo, w, b in ((0, 256, "p0"), (256, 128, "p1")):
        act(col(Fh, lo, w), col(Q, lo, w), AF.Copy, scale=1.0 / 16384, bias=UP14)
        for c in range(lo, lo + w, 128):
            o = col(b, c)
            mm(o, [(o, col(Fh, c), "N12K"), (o, "MONE", col("CP", c)), (o, col(Q, c), "EYE32")])
        cp("a", col("YP", lo, w), col(b, lo, w))
    op("s", lambda e: e.dma_start(T.yx[:], ap(("X", 0, 4096))), [("X", 0, 4096)], [("OUTX", 0, 1)], 0.06, kind="dma", bytes=1 << 20, tail=7.0)
    op("s", lambda e: e.dma_start(T.yp[:], ap("YP")), ["YP"], [("OUTP", 0, 1)], 0.06, kind="dma", bytes=128 * 384 * 4, tail=3.0)
    return ops
